import numpy as np
import ml_dtypes


def mxq(x, axis, fmt="e4m3"):
    dtype, down = {"e4m3": (ml_dtypes.float8_e4m3fn, 7), "e5m2": (ml_dtypes.float8_e5m2, 14)}[fmt]
    v = np.moveaxis(np.asarray(x, np.float32).astype(ml_dtypes.bfloat16).astype(np.float64), axis, -1)
    blocks = v.reshape(v.shape[:-1] + (-1, 32))
    amax = np.abs(blocks).max(-1, keepdims=True)
    byte = np.maximum(np.where(amax > 0, np.frexp(amax)[1] - 1 + 127, 0) - down, 1)
    scale = np.exp2(byte - 127.0)
    codes = (blocks / scale).astype(np.float32).astype(dtype).astype(np.float64)
    return np.moveaxis((codes * scale).reshape(v.shape), -1, axis)


WIDE = False


def mx_kscale(k):
    if not WIDE:
        return np.ones(k)
    levels = np.array([10, -10, 5, -5, 0])
    if k % 512:
        return np.exp2(np.random.permutation(np.resize(levels, k // 32))).repeat(32)
    a = np.empty((k // 512, 16))
    for p in range(k // 512):
        a[p, :8] = np.random.permutation(np.resize(levels, 8))
        for g in range(8):
            far = levels[np.abs(levels - a[p, g]) >= 10]
            a[p, g + 8] = far[np.random.randint(len(far))]
    return np.exp2(a.ravel()).repeat(32)


def f64(x):
    return np.asarray(x).astype(np.float64)


def striped(idx):
    return np.tile(idx.reshape(-1, 16).T, (8, 1)).astype(np.uint16)


def unstriped(offs):
    return offs[:16].T.reshape(-1).astype(np.int64)


def pack_weight(w):
    k, n = w.shape
    w = f64(np.asarray(w, np.float32).astype(ml_dtypes.bfloat16)).reshape(k // 32, 32, n)
    amax = np.abs(w).max(1)
    byte = np.clip(np.where(amax > 0, np.frexp(amax)[1] - 1 + 127 - 7, 1), 1, 254)
    scaled = (w * np.exp2(127.0 - byte)[:, None, :]).reshape(k, n).astype(np.float32)
    words = np.ascontiguousarray(scaled.reshape(k // 512, 128, 4, n).transpose(0, 1, 3, 2)).astype(ml_dtypes.float8_e4m3fn).view(np.uint8)
    return words, np.ascontiguousarray(byte.astype(np.uint8).reshape(k // 512, 16, n))


def unpack_weight(words, scales):
    g, p, n, _ = words.shape
    vals = np.ascontiguousarray(words).view(ml_dtypes.float8_e4m3fn).astype(np.float64) * np.repeat(np.exp2(scales.astype(np.float64) - 127.0), 8, axis=1)[..., None]
    return vals.transpose(0, 1, 3, 2).reshape(g * 512, n)


K, T, S, H, V, W = 512, 1024, 512, 512, 256, 1024
P = 2 ** 7


def setup_inputs():
    n = np.random.standard_normal
    s = mx_kscale(K)[:, None]
    u = mx_kscale(H)
    packed_xT = pack_weight(n((K, T)) * s)
    packed_eT = pack_weight(n((H, W)) / np.sqrt(H) / u[:, None])
    return {
        "x_words": packed_xT[0],
        "x_scales": packed_xT[1],
        "w1": (n((K, H)) / np.sqrt(K) / s * u).astype(np.float32),
        "e_words": packed_eT[0],
        "e_scales": packed_eT[1],
        "qn": (np.tile(np.random.uniform(1.5, 3.0, W), (P, 1))).astype(np.float32),
        "own": (np.random.uniform(1.5, 3.0, (S, 1))).astype(np.float32),
        "mass": (np.tile(np.random.uniform(0.5, 1.5, V), (P, 1))).astype(np.float32),
        "offs": striped(np.random.permutation(T)[:S]),
        "cen": striped(np.random.permutation(W)[:V]),
    }


def reference(x_words, x_scales, w1, e_words, e_scales, qn, own, mass, offs, cen):
    xq = unpack_weight(x_words, x_scales)[:, unstriped(offs)]
    h = mxq(f64(w1), 0, "e4m3").T @ xq
    e_cen = unpack_weight(e_words, e_scales)[:, unstriped(cen)]
    y = mxq(h, 0, "e4m3").T @ e_cen
    dd = f64(qn)[:1][:, unstriped(cen)] - (0.2 * y) + f64(own)
    gg = f64(mass)[:1] / (dd + 1.0)
    total = gg.sum(axis=1, keepdims=True)
    return gg / total

@@ -1,0 +1,155 @@
+from contextlib import ExitStack
+
+import concourse.mybir as mybir
+
+F32 = mybir.dt.float32
+BF16 = mybir.dt.bfloat16
+I32 = mybir.dt.int32
+U32 = mybir.dt.uint32
+U16 = mybir.dt.uint16
+U8 = mybir.dt.uint8
+FP8X4 = mybir.dt.float8_e4m3fn_x4
+ALU = mybir.AluOpType
+ACT = mybir.ActivationFunctionType
+
+P = 128
+PACK = 4
+K, T, S, H, V, W = 512, 1024, 512, 512, 256, 1024
+TILES = S // P
+HALF = H // 2
+
+FLOPS = 2 * K * H * S + 2 * H * S * V
+
+
+def load_scales(nc, queue, plane, scales):
+    for q in range(4):
+        queue.dma_start(out=plane[32 * q : 32 * q + 4, :].bitcast(I32), in_=scales[0, 4 * q : 4 * q + 4, :].bitcast(I32))
+
+
+def tile_picked_ydec_as_p_kernel(
+    tc, x_words, x_scales, w1, e_words, e_scales, qn, own, mass, offs, cen, out
+):
+    nc = tc.nc
+    with ExitStack() as ctx:
+        keep = ctx.enter_context(tc.tile_pool(name="keep", bufs=1))
+        psum = ctx.enter_context(tc.psum_pool(name="psum", bufs=1))
+
+        offs_t = keep.tile([P, S // 16], U16, name="offs_t")
+        cen_t = keep.tile([P, V // 16], U16, name="cen_t")
+        x_tab = keep.tile([P, T], I32, name="x_tab")
+        e_tab = keep.tile([P, W], I32, name="e_tab")
+        x_plane = keep.tile([P, T], U8, name="x_plane")
+        e_plane = keep.tile([P, W], U8, name="e_plane")
+        qn_tab = keep.tile([P, W], F32, name="qn_tab")
+        mass_t = keep.tile([P, V], F32, name="mass_t")
+        own_t = keep.tile([P, TILES], F32, name="own_t")
+        w_raw = [keep.tile([P, PACK, HALF], F32, name="w_raw%d" % i) for i in range(2)]
+
+        nc.vector.memset(x_plane[:].bitcast(I32), 0)
+        nc.vector.memset(e_plane[:].bitcast(I32), 0)
+        warm_in = keep.tile([P, 1], F32, name="warm_in")
+        warm_out = keep.tile([P, 1], F32, name="warm_out")
+        nc.vector.memset(warm_in[:], 1.0)
+
+        nc.sync.dma_start(offs_t[:], offs)
+        nc.sync.dma_start(cen_t[:], cen)
+        nc.sync.dma_start(out=x_tab[:], in_=x_words[0].rearrange("p n t -> p (n t)").bitcast(I32))
+        load_scales(nc, nc.scalar, x_plane, x_scales)
+        nc.scalar.activation(out=warm_out[:], in_=warm_in[:], func=ACT.Abs_reciprocal_sqrt)
+        w_rows = w1.rearrange("(p j) c -> p j c", j=PACK)
+        for i in range(2):
+            nc.sync.dma_start(out=w_raw[i][:], in_=w_rows[:, :, i * HALF : (i + 1) * HALF])
+        load_scales(nc, nc.scalar, e_plane, e_scales)
+        nc.sync.dma_start(out=e_tab[:], in_=e_words[0].rearrange("p n t -> p (n t)").bitcast(I32))
+        nc.sync.dma_start(out=qn_tab[:], in_=qn)
+        with nc.allow_non_contiguous_dma(reason="one value a partition for each tile of samples"):
+            nc.sync.dma_start(out=own_t[:], in_=own.rearrange("(n p) o -> p (n o)", p=P))
+        nc.sync.dma_start(out=mass_t[:], in_=mass)
+
+        x_codes = keep.tile([P, S], U32, name="x_codes", align_bytes=64)
+        x_sc = keep.tile([P, S], U8, name="x_sc", align_bytes=64)
+        e_codes = keep.tile([P, V], U32, name="e_codes", align_bytes=64)
+        e_sc = keep.tile([P, V], U8, name="e_sc", align_bytes=64)
+        nc.vector.tensor_copy(x_sc[:], x_plane[:].indirect(offs_t[:]))
+        nc.vector.tensor_copy(x_codes[:], x_tab[:].bitcast(U32).indirect(offs_t[:]))
+        nc.vector.tensor_copy(e_sc[:], e_plane[:].indirect(cen_t[:]))
+
+        w_bf = keep.tile([P, PACK, P, PACK], BF16, name="w_bf", align_bytes=64)
+        w_dst = w_bf[:].rearrange("p t m j -> p m t j")
+        nc.scalar.copy(out=w_dst[:, 0:64], in_=w_raw[0][:].rearrange("p j (m t) -> p m t j", t=PACK))
+        src1 = w_raw[1][:].rearrange("p j (m t) -> p m t j", t=PACK)
+        nc.scalar.copy(out=w_dst[:, 64:88], in_=src1[:, 0:24])
+        nc.vector.tensor_copy(out=w_dst[:, 88:128], in_=src1[:, 24:64])
+
+        w_codes = [keep.tile([P, P], U32, name="w_codes%d" % t, align_bytes=64) for t in range(PACK)]
+        w_sc = [keep.tile([P, P], U8, name="w_sc%d" % t, align_bytes=64) for t in range(PACK)]
+        for t in range(PACK):
+            nc.vector.quantize_mx(
+                out=w_codes[t][:].bitcast(FP8X4), scales=w_sc[t][:], in_=w_bf[:, t].rearrange("p m j -> p (m j)")
+            )
+
+        nc.vector.tensor_copy(e_codes[:], e_tab[:].bitcast(U32).indirect(cen_t[:]))
+
+        h_bf = []
+        for n in range(TILES):
+            cols = slice(n * P, (n + 1) * P)
+            h_ps = psum.tile([P, PACK, P], F32, name="h_ps%d" % n)
+            for t in range(PACK):
+                nc.tensor.matmul_mx(
+                    out=h_ps[:, t, :],
+                    lhsT=w_codes[t][:].bitcast(FP8X4),
+                    lhsT_scale=w_sc[t][:],
+                    rhs=x_codes[:, cols].bitcast(FP8X4),
+                    rhs_scale=x_sc[:, cols],
+                    start=True,
+                    stop=True,
+                )
+            hb = keep.tile([P, P, PACK], BF16, name="h_bf%d" % n, align_bytes=64)
+            nc.scalar.copy(out=hb[:], in_=h_ps[:].rearrange("p t n -> p n t"))
+            h_bf.append(hb)
+
+        q_cen = keep.tile([P, V], F32, name="q_cen")
+        q5 = keep.tile([P, V], F32, name="q5")
+        shift = keep.tile([P, TILES], F32, name="shift")
+        nc.vector.tensor_copy(q_cen[:], qn_tab[:].indirect(cen_t[:]))
+        nc.vector.tensor_scalar(shift[:], own_t[:], -5.0, -5.0, ALU.mult, ALU.add)
+        nc.vector.tensor_scalar(q5[:], q_cen[:], 5.0, None, ALU.mult)
+
+        den = []
+        for n in range(TILES):
+            h_codes = keep.tile([P, P], U32, name="h_codes%d" % n, align_bytes=64)
+            h_sc = keep.tile([P, P], U8, name="h_sc%d" % n, align_bytes=64)
+            nc.vector.quantize_mx(
+                out=h_codes[:].bitcast(FP8X4), scales=h_sc[:], in_=h_bf[n][:].rearrange("p n t -> p (n t)")
+            )
+            y = psum.tile([P, V], F32, name="y_ps%d" % n)
+            nc.tensor.matmul_mx(
+                out=y[:],
+                lhsT=h_codes[:].bitcast(FP8X4),
+                lhsT_scale=h_sc[:],
+                rhs=e_codes[:].bitcast(FP8X4),
+                rhs_scale=e_sc[:],
+                start=True,
+                stop=True,
+            )
+            d = keep.tile([P, V], F32, name="den%d" % n)
+            nc.vector.scalar_tensor_tensor(d[:], y[:], shift[:, n : n + 1], q5[:], ALU.add, ALU.subtract)
+            den.append(d)
+
+        for n in range(TILES):
+            root = keep.tile([P, V], F32, name="root%d" % n)
+            inv = keep.tile([P, V], F32, name="inv%d" % n)
+            sgn = keep.tile([P, V], F32, name="sgn%d" % n)
+            smass = keep.tile([P, V], F32, name="smass%d" % n)
+            gg = keep.tile([P, V], F32, name="gg%d" % n)
+            res = keep.tile([P, V], F32, name="res%d" % n)
+            total = keep.tile([P, 1], F32, name="total%d" % n)
+            rtotal = keep.tile([P, 1], F32, name="rtotal%d" % n)
+            nc.scalar.activation(out=root[:], in_=den[n][:], func=ACT.Abs_reciprocal_sqrt)
+            nc.scalar.activation(out=sgn[:], in_=den[n][:], func=ACT.Sign)
+            nc.scalar.activation(out=inv[:], in_=root[:], func=ACT.Square)
+            nc.vector.tensor_tensor(smass[:], sgn[:], mass_t[:], ALU.mult)
+            nc.vector.scalar_tensor_tensor(gg[:], inv[:], 1.0, smass[:], ALU.mult, ALU.mult, accum_out=total[:])
+            nc.vector.reciprocal(rtotal[:], total[:])
+            nc.vector.tensor_scalar(res[:], gg[:], rtotal[:], None, ALU.mult)
+            nc.sync.dma_start(out=out[n * P : (n + 1) * P, :], in_=res[:])

@@ -32,6 +32,7 @@ def tile_picked_ydec_as_p_kernel(
     nc = tc.nc
     with ExitStack() as ctx:
         keep = ctx.enter_context(tc.tile_pool(name="keep", bufs=1))
+        reuse = ctx.enter_context(tc.tile_pool(name="reuse", bufs=1))
         psum = ctx.enter_context(tc.psum_pool(name="psum", bufs=1))
 
         offs_t = keep.tile([P, S // 16], U16, name="offs_t")
@@ -39,57 +40,58 @@ def tile_picked_ydec_as_p_kernel(
         x_tab = keep.tile([P, T], I32, name="x_tab")
         e_tab = keep.tile([P, W], I32, name="e_tab")
         x_plane = keep.tile([P, T], U8, name="x_plane")
-        e_plane = keep.tile([P, W], U8, name="e_plane")
-        qn_tab = keep.tile([P, W], F32, name="qn_tab")
+        e_plane = reuse.tile([P, W], U8, name="e_plane", align_bytes=64, offset=7168)
+        qn_tab = reuse.tile([P, W], F32, name="qn_tab", align_bytes=64, offset=3072)
         mass_t = keep.tile([P, V], F32, name="mass_t")
         own_t = keep.tile([P, TILES], F32, name="own_t")
         w_raw = [keep.tile([P, PACK, HALF], F32, name="w_raw%d" % i) for i in range(2)]
 
         nc.vector.memset(x_plane[:].bitcast(I32), 0)
-        nc.vector.memset(e_plane[:].bitcast(I32), 0)
+        nc.gpsimd.memset(e_plane[:].bitcast(I32), 0)
         warm_in = keep.tile([P, 1], F32, name="warm_in")
         warm_out = keep.tile([P, 1], F32, name="warm_out")
         nc.vector.memset(warm_in[:], 1.0)
-
-        nc.sync.dma_start(offs_t[:], offs)
-        nc.sync.dma_start(cen_t[:], cen)
-        nc.sync.dma_start(out=x_tab[:], in_=x_words[0].rearrange("p n t -> p (n t)").bitcast(I32))
-        load_scales(nc, nc.scalar, x_plane, x_scales)
-        nc.scalar.activation(out=warm_out[:], in_=warm_in[:], func=ACT.Abs_reciprocal_sqrt)
         w_rows = w1.rearrange("(p j) c -> p j c", j=PACK)
-        for i in range(2):
-            nc.sync.dma_start(out=w_raw[i][:], in_=w_rows[:, :, i * HALF : (i + 1) * HALF])
-        load_scales(nc, nc.scalar, e_plane, e_scales)
+        nc.scalar.activation(out=warm_out[:], in_=warm_in[:], func=ACT.Abs_reciprocal_sqrt)
+        nc.sync.dma_start(offs_t[:], offs)
+        nc.sync.dma_start(out=x_tab[:], in_=x_words[0].rearrange("p n t -> p (n t)").bitcast(I32))
+        nc.sync.dma_start(cen_t[:], cen)
+        load_scales(nc, nc.sync, x_plane, x_scales)
+        nc.sync.dma_start(out=w_raw[0][:], in_=w_rows[:, :, 0:HALF])
+        nc.sync.dma_start(out=w_raw[1][:], in_=w_rows[:, :, HALF:H])
         nc.sync.dma_start(out=e_tab[:], in_=e_words[0].rearrange("p n t -> p (n t)").bitcast(I32))
+        load_scales(nc, nc.sync, e_plane, e_scales)
+        nc.sync.dma_start(out=mass_t[:], in_=mass)
         nc.sync.dma_start(out=qn_tab[:], in_=qn)
         with nc.allow_non_contiguous_dma(reason="one value a partition for each tile of samples"):
             nc.sync.dma_start(out=own_t[:], in_=own.rearrange("(n p) o -> p (n o)", p=P))
-        nc.sync.dma_start(out=mass_t[:], in_=mass)
-
         x_codes = keep.tile([P, S], U32, name="x_codes", align_bytes=64)
         x_sc = keep.tile([P, S], U8, name="x_sc", align_bytes=64)
-        e_codes = keep.tile([P, V], U32, name="e_codes", align_bytes=64)
-        e_sc = keep.tile([P, V], U8, name="e_sc", align_bytes=64)
-        nc.vector.tensor_copy(x_sc[:], x_plane[:].indirect(offs_t[:]))
         nc.vector.tensor_copy(x_codes[:], x_tab[:].bitcast(U32).indirect(offs_t[:]))
-        nc.vector.tensor_copy(e_sc[:], e_plane[:].indirect(cen_t[:]))
-
-        w_bf = keep.tile([P, PACK, P, PACK], BF16, name="w_bf", align_bytes=64)
-        w_dst = w_bf[:].rearrange("p t m j -> p m t j")
-        nc.scalar.copy(out=w_dst[:, 0:64], in_=w_raw[0][:].rearrange("p j (m t) -> p m t j", t=PACK))
-        src1 = w_raw[1][:].rearrange("p j (m t) -> p m t j", t=PACK)
-        nc.scalar.copy(out=w_dst[:, 64:88], in_=src1[:, 0:24])
-        nc.vector.tensor_copy(out=w_dst[:, 88:128], in_=src1[:, 24:64])
-
+        nc.vector.tensor_copy(x_sc[:], x_plane[:].indirect(offs_t[:]))
         w_codes = [keep.tile([P, P], U32, name="w_codes%d" % t, align_bytes=64) for t in range(PACK)]
         w_sc = [keep.tile([P, P], U8, name="w_sc%d" % t, align_bytes=64) for t in range(PACK)]
+        w_bf = keep.tile([P, PACK, 64, PACK], BF16, name="w_bf0", align_bytes=64)
+        w_dst = w_bf[:].rearrange("p t m j -> p m t j")
+        w_src = w_raw[0][:].rearrange("p j (m t) -> p m t j", t=PACK)
+        nc.scalar.copy(out=w_dst[:, 0:64], in_=w_src[:, 0:64])
         for t in range(PACK):
-            nc.vector.quantize_mx(
-                out=w_codes[t][:].bitcast(FP8X4), scales=w_sc[t][:], in_=w_bf[:, t].rearrange("p m j -> p (m j)")
-            )
-
+            nc.vector.quantize_mx(out=w_codes[t][:, 0:64].bitcast(FP8X4), scales=w_sc[t][:, 0:64], in_=w_bf[:, t].rearrange("p m j -> p (m j)"))
+        w_bf = reuse.tile([P, PACK, 64, PACK], BF16, name="w_bf1", align_bytes=64, offset=768)
+        w_dst = w_bf[:].rearrange("p t m j -> p m t j")
+        w_src = w_raw[1][:].rearrange("p j (m t) -> p m t j", t=PACK)
+        nc.scalar.copy(out=w_dst[:, 0:28], in_=w_src[:, 0:28])
+        nc.vector.tensor_copy(out=w_dst[:, 28:64], in_=w_src[:, 28:64])
+        for t in range(PACK):
+            nc.vector.quantize_mx(out=w_codes[t][:, 64:128].bitcast(FP8X4), scales=w_sc[t][:, 64:128], in_=w_bf[:, t].rearrange("p m j -> p (m j)"))
+        e_codes = reuse.tile([P, V], U32, name="e_codes", align_bytes=64, offset=0)
+        e_sc = reuse.tile([P, V], U8, name="e_sc", align_bytes=64, offset=1024)
         nc.vector.tensor_copy(e_codes[:], e_tab[:].bitcast(U32).indirect(cen_t[:]))
-
+        nc.vector.tensor_copy(e_sc[:], e_plane[:].indirect(cen_t[:]))
+        q_cen = reuse.tile([P, V], F32, name="q_cen", align_bytes=64, offset=1280)
+        nc.vector.tensor_copy(q_cen[:], qn_tab[:].indirect(cen_t[:]))
+        own1 = keep.tile([P, TILES], F32, name="own1")
+        nc.gpsimd.tensor_scalar(own1[:], own_t[:], 1.0, 1.0, ALU.mult, ALU.add)
         h_bf = []
         for n in range(TILES):
             cols = slice(n * P, (n + 1) * P)
@@ -104,21 +106,21 @@ def tile_picked_ydec_as_p_kernel(
                     start=True,
                     stop=True,
                 )
-            hb = keep.tile([P, P, PACK], BF16, name="h_bf%d" % n, align_bytes=64)
+            if n >= 2:
+                hb = reuse.tile([P, P, PACK], BF16, name="h_bf%d" % n, align_bytes=64, offset=3072 + 1024 * (n - 2))
+            else:
+                hb = keep.tile([P, P, PACK], BF16, name="h_bf%d" % n, align_bytes=64)
             nc.scalar.copy(out=hb[:], in_=h_ps[:].rearrange("p t n -> p n t"))
             h_bf.append(hb)
 
-        q_cen = keep.tile([P, V], F32, name="q_cen")
-        q5 = keep.tile([P, V], F32, name="q5")
-        shift = keep.tile([P, TILES], F32, name="shift")
-        nc.vector.tensor_copy(q_cen[:], qn_tab[:].indirect(cen_t[:]))
-        nc.vector.tensor_scalar(shift[:], own_t[:], -5.0, -5.0, ALU.mult, ALU.add)
-        nc.vector.tensor_scalar(q5[:], q_cen[:], 5.0, None, ALU.mult)
-
         den = []
         for n in range(TILES):
-            h_codes = keep.tile([P, P], U32, name="h_codes%d" % n, align_bytes=64)
-            h_sc = keep.tile([P, P], U8, name="h_sc%d" % n, align_bytes=64)
+            if n < 2:
+                h_codes = reuse.tile([P, P], U32, name="h_codes%d" % n, align_bytes=64, offset=5120 + 512 * n)
+                h_sc = reuse.tile([P, P], U8, name="h_sc%d" % n, align_bytes=64, offset=7168 + 128 * n)
+            else:
+                h_codes = keep.tile([P, P], U32, name="h_codes%d" % n, align_bytes=64)
+                h_sc = keep.tile([P, P], U8, name="h_sc%d" % n, align_bytes=64)
             nc.vector.quantize_mx(
                 out=h_codes[:].bitcast(FP8X4), scales=h_sc[:], in_=h_bf[n][:].rearrange("p n t -> p (n t)")
             )
@@ -133,7 +135,7 @@ def tile_picked_ydec_as_p_kernel(
                 stop=True,
             )
             d = keep.tile([P, V], F32, name="den%d" % n)
-            nc.vector.scalar_tensor_tensor(d[:], y[:], shift[:, n : n + 1], q5[:], ALU.add, ALU.subtract)
+            nc.vector.scalar_tensor_tensor(d[:], y[:], -0.2, q_cen[:], ALU.mult, ALU.add)
             den.append(d)
 
         for n in range(TILES):
@@ -145,11 +147,20 @@ def tile_picked_ydec_as_p_kernel(
             res = keep.tile([P, V], F32, name="res%d" % n)
             total = keep.tile([P, 1], F32, name="total%d" % n)
             rtotal = keep.tile([P, 1], F32, name="rtotal%d" % n)
-            nc.scalar.activation(out=root[:], in_=den[n][:], func=ACT.Abs_reciprocal_sqrt)
-            nc.scalar.activation(out=sgn[:], in_=den[n][:], func=ACT.Sign)
-            nc.scalar.activation(out=inv[:], in_=root[:], func=ACT.Square)
-            nc.vector.tensor_tensor(smass[:], sgn[:], mass_t[:], ALU.mult)
+            bias = own1[:, n : n + 1]
+            nc.scalar.activation(out=root[:], in_=den[n][:], func=ACT.Abs_reciprocal_sqrt, bias=bias)
+            if n >= 2:
+                nc.vector.tensor_scalar(sgn[:], den[n][:], bias, 0.0, ALU.add, ALU.is_ge)
+                nc.scalar.activation(out=inv[:], in_=root[:], func=ACT.Square)
+                nc.vector.scalar_tensor_tensor(smass[:], sgn[:], 0.5, mass_t[:], ALU.subtract, ALU.mult)
+            else:
+                nc.scalar.activation(out=sgn[:], in_=den[n][:], func=ACT.Sign, bias=bias)
+                nc.scalar.activation(out=inv[:], in_=root[:], func=ACT.Square)
+                nc.vector.tensor_tensor(smass[:], sgn[:], mass_t[:], ALU.mult)
             nc.vector.scalar_tensor_tensor(gg[:], inv[:], 1.0, smass[:], ALU.mult, ALU.mult, accum_out=total[:])
             nc.vector.reciprocal(rtotal[:], total[:])
-            nc.vector.tensor_scalar(res[:], gg[:], rtotal[:], None, ALU.mult)
+            if n < 3:
+                nc.scalar.activation(out=res[:], in_=gg[:], func=ACT.Copy, scale=rtotal[:])
+            else:
+                nc.vector.tensor_scalar(res[:], gg[:], rtotal[:], None, ALU.mult)
             nc.sync.dma_start(out=out[n * P : (n + 1) * P, :], in_=res[:])

@@ -47,22 +47,22 @@ def tile_picked_ydec_as_p_kernel(
         w_raw = [keep.tile([P, PACK, HALF], F32, name="w_raw%d" % i) for i in range(2)]
 
         nc.vector.memset(x_plane[:].bitcast(I32), 0)
-        nc.gpsimd.memset(e_plane[:].bitcast(I32), 0)
+        nc.vector.memset(e_plane[:].bitcast(I32), 0)
         warm_in = keep.tile([P, 1], F32, name="warm_in")
         warm_out = keep.tile([P, 1], F32, name="warm_out")
         nc.vector.memset(warm_in[:], 1.0)
         w_rows = w1.rearrange("(p j) c -> p j c", j=PACK)
         nc.scalar.activation(out=warm_out[:], in_=warm_in[:], func=ACT.Abs_reciprocal_sqrt)
-        nc.sync.dma_start(offs_t[:], offs)
         nc.sync.dma_start(out=x_tab[:], in_=x_words[0].rearrange("p n t -> p (n t)").bitcast(I32))
-        nc.sync.dma_start(cen_t[:], cen)
+        nc.sync.dma_start(offs_t[:], offs)
         load_scales(nc, nc.sync, x_plane, x_scales)
         nc.sync.dma_start(out=w_raw[0][:], in_=w_rows[:, :, 0:HALF])
         nc.sync.dma_start(out=w_raw[1][:], in_=w_rows[:, :, HALF:H])
+        nc.sync.dma_start(cen_t[:], cen)
         nc.sync.dma_start(out=e_tab[:], in_=e_words[0].rearrange("p n t -> p (n t)").bitcast(I32))
         load_scales(nc, nc.sync, e_plane, e_scales)
-        nc.sync.dma_start(out=mass_t[:], in_=mass)
         nc.sync.dma_start(out=qn_tab[:], in_=qn)
+        nc.sync.dma_start(out=mass_t[:], in_=mass)
         with nc.allow_non_contiguous_dma(reason="one value a partition for each tile of samples"):
             nc.sync.dma_start(out=own_t[:], in_=own.rearrange("(n p) o -> p (n o)", p=P))
         x_codes = keep.tile([P, S], U32, name="x_codes", align_bytes=64)
@@ -72,14 +72,14 @@ def tile_picked_ydec_as_p_kernel(
         w_codes = [keep.tile([P, P], U32, name="w_codes%d" % t, align_bytes=64) for t in range(PACK)]
         w_sc = [keep.tile([P, P], U8, name="w_sc%d" % t, align_bytes=64) for t in range(PACK)]
         w_bf = keep.tile([P, PACK, 64, PACK], BF16, name="w_bf0", align_bytes=64)
-        w_dst = w_bf[:].rearrange("p t m j -> p m t j")
-        w_src = w_raw[0][:].rearrange("p j (m t) -> p m t j", t=PACK)
+        w_dst = w_bf[:].rearrange("p t m j -> p m j t")
+        w_src = w_raw[0][:].rearrange("p j (m t) -> p m j t", t=PACK)
         nc.scalar.copy(out=w_dst[:, 0:64], in_=w_src[:, 0:64])
         for t in range(PACK):
             nc.vector.quantize_mx(out=w_codes[t][:, 0:64].bitcast(FP8X4), scales=w_sc[t][:, 0:64], in_=w_bf[:, t].rearrange("p m j -> p (m j)"))
         w_bf = reuse.tile([P, PACK, 64, PACK], BF16, name="w_bf1", align_bytes=64, offset=768)
-        w_dst = w_bf[:].rearrange("p t m j -> p m t j")
-        w_src = w_raw[1][:].rearrange("p j (m t) -> p m t j", t=PACK)
+        w_dst = w_bf[:].rearrange("p t m j -> p m j t")
+        w_src = w_raw[1][:].rearrange("p j (m t) -> p m j t", t=PACK)
         nc.scalar.copy(out=w_dst[:, 0:28], in_=w_src[:, 0:28])
         nc.vector.tensor_copy(out=w_dst[:, 28:64], in_=w_src[:, 28:64])
         for t in range(PACK):

@@ -91,7 +91,7 @@ def tile_picked_ydec_as_p_kernel(
         q_cen = reuse.tile([P, V], F32, name="q_cen", align_bytes=64, offset=1280)
         nc.vector.tensor_copy(q_cen[:], qn_tab[:].indirect(cen_t[:]))
         own1 = keep.tile([P, TILES], F32, name="own1")
-        nc.gpsimd.tensor_scalar(own1[:], own_t[:], 1.0, 1.0, ALU.mult, ALU.add)
+        nc.scalar.activation(out=own1[:], in_=own_t[:], func=ACT.Copy, bias=1.0)
         h_bf = []
         for n in range(TILES):
             cols = slice(n * P, (n + 1) * P)
@@ -110,7 +110,9 @@ def tile_picked_ydec_as_p_kernel(
                 hb = reuse.tile([P, P, PACK], BF16, name="h_bf%d" % n, align_bytes=64, offset=3072 + 1024 * (n - 2))
             else:
                 hb = keep.tile([P, P, PACK], BF16, name="h_bf%d" % n, align_bytes=64)
-            nc.scalar.copy(out=hb[:], in_=h_ps[:].rearrange("p t n -> p n t"))
+            nc.scalar.copy(
+                out=hb[:].rearrange("p (c i) t -> p c t i", i=2), in_=h_ps[:].rearrange("p t (c i) -> p c t i", i=2)
+            )
             h_bf.append(hb)
 
         den = []

@@ -80,11 +80,11 @@ def tile_picked_ydec_as_p_kernel(
         w_bf = reuse.tile([P, PACK, 64, PACK], BF16, name="w_bf1", align_bytes=64, offset=768)
         w_dst = w_bf[:].rearrange("p t m j -> p m j t")
         w_src = w_raw[1][:].rearrange("p j (m t) -> p m j t", t=PACK)
-        nc.scalar.copy(out=w_dst[:, 0:28], in_=w_src[:, 0:28])
-        nc.vector.tensor_copy(out=w_dst[:, 28:64], in_=w_src[:, 28:64])
+        nc.scalar.copy(out=w_dst[:, 0:20], in_=w_src[:, 0:20])
+        nc.vector.tensor_copy(out=w_dst[:, 20:64], in_=w_src[:, 20:64])
         for t in range(PACK):
             nc.vector.quantize_mx(out=w_codes[t][:, 64:128].bitcast(FP8X4), scales=w_sc[t][:, 64:128], in_=w_bf[:, t].rearrange("p m j -> p (m j)"))
-        e_codes = reuse.tile([P, V], U32, name="e_codes", align_bytes=64, offset=0)
+        e_codes = keep.tile([P, V], U32, name="e_codes", align_bytes=64)
         e_sc = reuse.tile([P, V], U8, name="e_sc", align_bytes=64, offset=1024)
         nc.vector.tensor_copy(e_codes[:], e_tab[:].bitcast(U32).indirect(cen_t[:]))
         nc.vector.tensor_copy(e_sc[:], e_plane[:].indirect(cen_t[:]))
@@ -116,6 +116,7 @@ def tile_picked_ydec_as_p_kernel(
             h_bf.append(hb)
 
         den = []
+        done = []
         for n in range(TILES):
             if n < 2:
                 h_codes = reuse.tile([P, P], U32, name="h_codes%d" % n, align_bytes=64, offset=5120 + 512 * n)
@@ -141,12 +142,14 @@ def tile_picked_ydec_as_p_kernel(
             den.append(d)
 
         for n in range(TILES):
-            root = keep.tile([P, V], F32, name="root%d" % n)
+            if n == TILES - 1:
+                root = reuse.tile([P, V], F32, name="root%d" % n, align_bytes=64, offset=9216 + 512)
+            else:
+                root = keep.tile([P, V], F32, name="root%d" % n)
             inv = keep.tile([P, V], F32, name="inv%d" % n)
             sgn = keep.tile([P, V], F32, name="sgn%d" % n)
             smass = keep.tile([P, V], F32, name="smass%d" % n)
             gg = keep.tile([P, V], F32, name="gg%d" % n)
-            res = keep.tile([P, V], F32, name="res%d" % n)
             total = keep.tile([P, 1], F32, name="total%d" % n)
             rtotal = keep.tile([P, 1], F32, name="rtotal%d" % n)
             bias = own1[:, n : n + 1]
@@ -161,6 +164,14 @@ def tile_picked_ydec_as_p_kernel(
                 nc.vector.tensor_tensor(smass[:], sgn[:], mass_t[:], ALU.mult)
             nc.vector.scalar_tensor_tensor(gg[:], inv[:], 1.0, smass[:], ALU.mult, ALU.mult, accum_out=total[:])
             nc.vector.reciprocal(rtotal[:], total[:])
+            done.append((gg, rtotal))
+
+        for n in range(TILES):
+            gg, rtotal = done[n]
+            if n < 2:
+                res = reuse.tile([P, V], F32, name="res%d" % n, align_bytes=64, offset=9216 + 1024 * n)
+            else:
+                res = keep.tile([P, V], F32, name="res%d" % n)
             if n < 3:
                 nc.scalar.activation(out=res[:], in_=gg[:], func=ACT.Copy, scale=rtotal[:])
             else:

@@ -17,6 +17,7 @@ PACK = 4
 K, T, S, H, V, W = 512, 1024, 512, 512, 256, 1024
 TILES = S // P
 HALF = H // 2
+BANK = 2048
 
 FLOPS = 2 * K * H * S + 2 * H * S * V
 
@@ -69,6 +70,16 @@ def tile_picked_ydec_as_p_kernel(
         x_sc = keep.tile([P, S], U8, name="x_sc", align_bytes=64)
         nc.vector.tensor_copy(x_codes[:], x_tab[:].bitcast(U32).indirect(offs_t[:]))
         nc.vector.tensor_copy(x_sc[:], x_plane[:].indirect(offs_t[:]))
+        warm_ps = psum.tile([P, S], F32, name="warm_ps", offset=(2 * TILES - 1) * BANK)
+        nc.tensor.matmul_mx(
+            out=warm_ps[:],
+            lhsT=x_codes[:, 0:P].bitcast(FP8X4),
+            lhsT_scale=x_sc[:, 0:P],
+            rhs=x_codes[:].bitcast(FP8X4),
+            rhs_scale=x_sc[:],
+            start=True,
+            stop=True,
+        )
         w_codes = [keep.tile([P, P], U32, name="w_codes%d" % t, align_bytes=64) for t in range(PACK)]
         w_sc = [keep.tile([P, P], U8, name="w_sc%d" % t, align_bytes=64) for t in range(PACK)]
         w_bf = keep.tile([P, PACK, 64, PACK], BF16, name="w_bf0", align_bytes=64)
@@ -95,7 +106,7 @@ def tile_picked_ydec_as_p_kernel(
         h_bf = []
         for n in range(TILES):
             cols = slice(n * P, (n + 1) * P)
-            h_ps = psum.tile([P, PACK, P], F32, name="h_ps%d" % n)
+            h_ps = psum.tile([P, PACK, P], F32, name="h_ps%d" % n, offset=n * BANK)
             for t in range(PACK):
                 nc.tensor.matmul_mx(
                     out=h_ps[:, t, :],
@@ -127,7 +138,7 @@ def tile_picked_ydec_as_p_kernel(
             nc.vector.quantize_mx(
                 out=h_codes[:].bitcast(FP8X4), scales=h_sc[:], in_=h_bf[n][:].rearrange("p n t -> p (n t)")
             )
-            y = psum.tile([P, V], F32, name="y_ps%d" % n)
+            y = psum.tile([P, V], F32, name="y_ps%d" % n, offset=(TILES + n) * BANK)
             nc.tensor.matmul_mx(
                 out=y[:],
                 lhsT=h_codes[:].bitcast(FP8X4),

@@ -17,12 +17,16 @@ PACK = 4
 K, T, S, H, V, W = 512, 1024, 512, 512, 256, 1024
 TILES = S // P
 HALF = H // 2
+GROUPS = HALF // PACK
 BANK = 2048
+SCALAR_GROUPS = 20
+SCALAR_SIGNS = 3
+SCALAR_SCALINGS = 3
 
 FLOPS = 2 * K * H * S + 2 * H * S * V
 
 
-def load_scales(nc, queue, plane, scales):
+def load_scales(queue, plane, scales):
     for q in range(4):
         queue.dma_start(out=plane[32 * q : 32 * q + 4, :].bitcast(I32), in_=scales[0, 4 * q : 4 * q + 4, :].bitcast(I32))
 
@@ -39,102 +43,94 @@ def tile_picked_ydec_as_p_kernel(
         offs_t = keep.tile([P, S // 16], U16, name="offs_t")
         cen_t = keep.tile([P, V // 16], U16, name="cen_t")
         x_tab = keep.tile([P, T], I32, name="x_tab")
-        e_tab = keep.tile([P, W], I32, name="e_tab")
         x_plane = keep.tile([P, T], U8, name="x_plane")
-        e_plane = reuse.tile([P, W], U8, name="e_plane", align_bytes=64, offset=7168)
-        qn_tab = reuse.tile([P, W], F32, name="qn_tab", align_bytes=64, offset=3072)
+        e_plane = keep.tile([P, W], U8, name="e_plane")
+        e_tab = reuse.tile([P, W], I32, name="e_tab", align_bytes=64, offset=0)
+        qn_tab = keep.tile([P, W], F32, name="qn_tab", align_bytes=64)
         mass_t = keep.tile([P, V], F32, name="mass_t")
-        own_t = keep.tile([P, TILES], F32, name="own_t")
+        own_t = reuse.tile([P, 64], F32, name="own_t", align_bytes=64, offset=4096)
         w_raw = [keep.tile([P, PACK, HALF], F32, name="w_raw%d" % i) for i in range(2)]
 
         nc.vector.memset(x_plane[:].bitcast(I32), 0)
-        nc.vector.memset(e_plane[:].bitcast(I32), 0)
         warm_in = keep.tile([P, 1], F32, name="warm_in")
         warm_out = keep.tile([P, 1], F32, name="warm_out")
         nc.vector.memset(warm_in[:], 1.0)
+        nc.vector.memset(e_plane[:].bitcast(I32), 0)
         w_rows = w1.rearrange("(p j) c -> p j c", j=PACK)
-        nc.scalar.activation(out=warm_out[:], in_=warm_in[:], func=ACT.Abs_reciprocal_sqrt)
-        nc.sync.dma_start(out=x_tab[:], in_=x_words[0].rearrange("p n t -> p (n t)").bitcast(I32))
-        nc.sync.dma_start(offs_t[:], offs)
-        load_scales(nc, nc.sync, x_plane, x_scales)
         nc.sync.dma_start(out=w_raw[0][:], in_=w_rows[:, :, 0:HALF])
+        nc.sync.dma_start(offs_t[:], offs)
+        load_scales(nc.scalar, x_plane, x_scales)
+        nc.scalar.activation(out=warm_out[:], in_=warm_in[:], func=ACT.Abs_reciprocal_sqrt)
         nc.sync.dma_start(out=w_raw[1][:], in_=w_rows[:, :, HALF:H])
-        nc.sync.dma_start(cen_t[:], cen)
+        nc.sync.dma_start(out=x_tab[:], in_=x_words[0].rearrange("p n t -> p (n t)").bitcast(I32))
         nc.sync.dma_start(out=e_tab[:], in_=e_words[0].rearrange("p n t -> p (n t)").bitcast(I32))
-        load_scales(nc, nc.sync, e_plane, e_scales)
+        load_scales(nc.sync, e_plane, e_scales)
+        nc.sync.dma_start(cen_t[:], cen)
         nc.sync.dma_start(out=qn_tab[:], in_=qn)
-        nc.sync.dma_start(out=mass_t[:], in_=mass)
         with nc.allow_non_contiguous_dma(reason="one value a partition for each tile of samples"):
-            nc.sync.dma_start(out=own_t[:], in_=own.rearrange("(n p) o -> p (n o)", p=P))
-        x_codes = keep.tile([P, S], U32, name="x_codes", align_bytes=64)
+            nc.sync.dma_start(out=own_t[:, 0:TILES], in_=own.rearrange("(n p) o -> p (n o)", p=P))
+        nc.sync.dma_start(out=mass_t[:], in_=mass)
+
         x_sc = keep.tile([P, S], U8, name="x_sc", align_bytes=64)
-        nc.vector.tensor_copy(x_codes[:], x_tab[:].bitcast(U32).indirect(offs_t[:]))
         nc.vector.tensor_copy(x_sc[:], x_plane[:].indirect(offs_t[:]))
-        warm_ps = psum.tile([P, S], F32, name="warm_ps", offset=(2 * TILES - 1) * BANK)
-        nc.tensor.matmul_mx(
-            out=warm_ps[:],
-            lhsT=x_codes[:, 0:P].bitcast(FP8X4),
-            lhsT_scale=x_sc[:, 0:P],
-            rhs=x_codes[:].bitcast(FP8X4),
-            rhs_scale=x_sc[:],
-            start=True,
-            stop=True,
-        )
+
         w_codes = [keep.tile([P, P], U32, name="w_codes%d" % t, align_bytes=64) for t in range(PACK)]
         w_sc = [keep.tile([P, P], U8, name="w_sc%d" % t, align_bytes=64) for t in range(PACK)]
-        w_bf = keep.tile([P, PACK, 64, PACK], BF16, name="w_bf0", align_bytes=64)
-        w_dst = w_bf[:].rearrange("p t m j -> p m j t")
-        w_src = w_raw[0][:].rearrange("p j (m t) -> p m j t", t=PACK)
-        nc.scalar.copy(out=w_dst[:, 0:64], in_=w_src[:, 0:64])
-        for t in range(PACK):
-            nc.vector.quantize_mx(out=w_codes[t][:, 0:64].bitcast(FP8X4), scales=w_sc[t][:, 0:64], in_=w_bf[:, t].rearrange("p m j -> p (m j)"))
-        w_bf = reuse.tile([P, PACK, 64, PACK], BF16, name="w_bf1", align_bytes=64, offset=768)
-        w_dst = w_bf[:].rearrange("p t m j -> p m j t")
-        w_src = w_raw[1][:].rearrange("p j (m t) -> p m j t", t=PACK)
-        nc.scalar.copy(out=w_dst[:, 0:20], in_=w_src[:, 0:20])
-        nc.vector.tensor_copy(out=w_dst[:, 20:64], in_=w_src[:, 20:64])
-        for t in range(PACK):
-            nc.vector.quantize_mx(out=w_codes[t][:, 64:128].bitcast(FP8X4), scales=w_sc[t][:, 64:128], in_=w_bf[:, t].rearrange("p m j -> p (m j)"))
+        w_bf = [keep.tile([P, PACK, GROUPS, PACK], BF16, name="w_bf%d" % i, align_bytes=64) for i in range(2)]
+        w_dst = [w_bf[i][:].rearrange("p t m j -> p m j t") for i in range(2)]
+        w_src = [w_raw[i][:].rearrange("p j (m t) -> p m j t", t=PACK) for i in range(2)]
+        nc.scalar.copy(out=w_dst[0], in_=w_src[0])
+        nc.scalar.copy(out=w_dst[1][:, 0:SCALAR_GROUPS], in_=w_src[1][:, 0:SCALAR_GROUPS])
+        nc.vector.tensor_copy(out=w_dst[1][:, SCALAR_GROUPS:GROUPS], in_=w_src[1][:, SCALAR_GROUPS:GROUPS])
+        for i in range(2):
+            cols = slice(i * GROUPS, (i + 1) * GROUPS)
+            for t in range(PACK):
+                nc.vector.quantize_mx(
+                    out=w_codes[t][:, cols].bitcast(FP8X4),
+                    scales=w_sc[t][:, cols],
+                    in_=w_bf[i][:, t].rearrange("p m j -> p (m j)"),
+                )
+
+        x_codes = []
+        for first, count in ((0, 1), (1, 1), (2, 2)):
+            picked = keep.tile([P, count * P], U32, name="x_codes%d" % first, align_bytes=64)
+            nc.vector.tensor_copy(picked[:], x_tab[:].bitcast(U32).indirect(offs_t[:, 8 * first : 8 * (first + count)]))
+            x_codes.extend(picked[:, i * P : (i + 1) * P] for i in range(count))
+
         e_codes = keep.tile([P, V], U32, name="e_codes", align_bytes=64)
-        e_sc = reuse.tile([P, V], U8, name="e_sc", align_bytes=64, offset=1024)
+        e_sc = keep.tile([P, V], U8, name="e_sc", align_bytes=64)
         nc.vector.tensor_copy(e_codes[:], e_tab[:].bitcast(U32).indirect(cen_t[:]))
         nc.vector.tensor_copy(e_sc[:], e_plane[:].indirect(cen_t[:]))
-        q_cen = reuse.tile([P, V], F32, name="q_cen", align_bytes=64, offset=1280)
-        nc.vector.tensor_copy(q_cen[:], qn_tab[:].indirect(cen_t[:]))
-        own1 = keep.tile([P, TILES], F32, name="own1")
-        nc.scalar.activation(out=own1[:], in_=own_t[:], func=ACT.Copy, bias=1.0)
+
         h_bf = []
         for n in range(TILES):
-            cols = slice(n * P, (n + 1) * P)
             h_ps = psum.tile([P, PACK, P], F32, name="h_ps%d" % n, offset=n * BANK)
             for t in range(PACK):
                 nc.tensor.matmul_mx(
                     out=h_ps[:, t, :],
                     lhsT=w_codes[t][:].bitcast(FP8X4),
                     lhsT_scale=w_sc[t][:],
-                    rhs=x_codes[:, cols].bitcast(FP8X4),
-                    rhs_scale=x_sc[:, cols],
+                    rhs=x_codes[n].bitcast(FP8X4),
+                    rhs_scale=x_sc[:, n * P : (n + 1) * P],
                     start=True,
                     stop=True,
                 )
-            if n >= 2:
-                hb = reuse.tile([P, P, PACK], BF16, name="h_bf%d" % n, align_bytes=64, offset=3072 + 1024 * (n - 2))
+            if n == 1:
+                hb = reuse.tile([P, P, PACK], BF16, name="h_bf%d" % n, align_bytes=64, offset=6144)
             else:
                 hb = keep.tile([P, P, PACK], BF16, name="h_bf%d" % n, align_bytes=64)
             nc.scalar.copy(
                 out=hb[:].rearrange("p (c i) t -> p c t i", i=2), in_=h_ps[:].rearrange("p t (c i) -> p c t i", i=2)
             )
             h_bf.append(hb)
+        own1 = keep.tile([P, TILES], F32, name="own1")
+        nc.gpsimd.tensor_scalar(own1[:], own_t[:, 0:TILES], 1.0, 1.0, ALU.mult, ALU.add)
 
-        den = []
-        done = []
-        for n in range(TILES):
-            if n < 2:
-                h_codes = reuse.tile([P, P], U32, name="h_codes%d" % n, align_bytes=64, offset=5120 + 512 * n)
-                h_sc = reuse.tile([P, P], U8, name="h_sc%d" % n, align_bytes=64, offset=7168 + 128 * n)
-            else:
-                h_codes = keep.tile([P, P], U32, name="h_codes%d" % n, align_bytes=64)
-                h_sc = keep.tile([P, P], U8, name="h_sc%d" % n, align_bytes=64)
+        y_ps = []
+
+        def second_product(n):
+            h_codes = keep.tile([P, P], U32, name="h_codes%d" % n, align_bytes=64)
+            h_sc = reuse.tile([P, P], U8, name="h_sc%d" % n, align_bytes=64, offset=(0, 4096, 6144, 6144 + 128)[n])
             nc.vector.quantize_mx(
                 out=h_codes[:].bitcast(FP8X4), scales=h_sc[:], in_=h_bf[n][:].rearrange("p n t -> p (n t)")
             )
@@ -148,43 +144,93 @@ def tile_picked_ydec_as_p_kernel(
                 start=True,
                 stop=True,
             )
-            d = keep.tile([P, V], F32, name="den%d" % n)
-            nc.vector.scalar_tensor_tensor(d[:], y[:], -0.2, q_cen[:], ALU.mult, ALU.add)
+            y_ps.append(y)
+
+        den = []
+
+        def denominator(n):
+            if n == 0:
+                d = reuse.tile([P, V], F32, name="den%d" % n, align_bytes=64, offset=4096 + 128)
+            else:
+                d = keep.tile([P, V], F32, name="den%d" % n)
+            nc.vector.scalar_tensor_tensor(d[:], y_ps[n][:], -0.2, q_cen[:], ALU.mult, ALU.add)
             den.append(d)
 
-        for n in range(TILES):
-            if n == TILES - 1:
-                root = reuse.tile([P, V], F32, name="root%d" % n, align_bytes=64, offset=9216 + 512)
-            else:
-                root = keep.tile([P, V], F32, name="root%d" % n)
-            inv = keep.tile([P, V], F32, name="inv%d" % n)
-            sgn = keep.tile([P, V], F32, name="sgn%d" % n)
-            smass = keep.tile([P, V], F32, name="smass%d" % n)
-            gg = keep.tile([P, V], F32, name="gg%d" % n)
-            total = keep.tile([P, 1], F32, name="total%d" % n)
-            rtotal = keep.tile([P, 1], F32, name="rtotal%d" % n)
-            bias = own1[:, n : n + 1]
-            nc.scalar.activation(out=root[:], in_=den[n][:], func=ACT.Abs_reciprocal_sqrt, bias=bias)
-            if n >= 2:
-                nc.vector.tensor_scalar(sgn[:], den[n][:], bias, 0.0, ALU.add, ALU.is_ge)
-                nc.scalar.activation(out=inv[:], in_=root[:], func=ACT.Square)
-                nc.vector.scalar_tensor_tensor(smass[:], sgn[:], 0.5, mass_t[:], ALU.subtract, ALU.mult)
-            else:
-                nc.scalar.activation(out=sgn[:], in_=den[n][:], func=ACT.Sign, bias=bias)
-                nc.scalar.activation(out=inv[:], in_=root[:], func=ACT.Square)
-                nc.vector.tensor_tensor(smass[:], sgn[:], mass_t[:], ALU.mult)
-            nc.vector.scalar_tensor_tensor(gg[:], inv[:], 1.0, smass[:], ALU.mult, ALU.mult, accum_out=total[:])
-            nc.vector.reciprocal(rtotal[:], total[:])
-            done.append((gg, rtotal))
+        second_product(0)
+        q_cen = keep.tile([P, V], F32, name="q_cen", align_bytes=64)
+        nc.vector.tensor_copy(q_cen[:], qn_tab[:].indirect(cen_t[:]))
+        second_product(1)
+        denominator(0)
+        second_product(2)
+        second_product(3)
+        for n in range(1, TILES):
+            denominator(n)
 
-        for n in range(TILES):
-            gg, rtotal = done[n]
+        root, inv, sgn, smass, gg, total, rtotal = {}, {}, {}, {}, {}, {}, {}
+
+        def inverse_root(n):
+            if n == TILES - 1:
+                root[n] = reuse.tile([P, V], F32, name="root%d" % n, align_bytes=64, offset=8192 + 512)
+            else:
+                root[n] = keep.tile([P, V], F32, name="root%d" % n)
+            nc.scalar.activation(out=root[n][:], in_=den[n][:], func=ACT.Abs_reciprocal_sqrt, bias=own1[:, n : n + 1])
+
+        def sign(n):
+            sgn[n] = keep.tile([P, V], F32, name="sgn%d" % n)
+            if n < SCALAR_SIGNS:
+                nc.scalar.activation(out=sgn[n][:], in_=den[n][:], func=ACT.Sign, bias=own1[:, n : n + 1])
+            else:
+                nc.vector.tensor_scalar(sgn[n][:], den[n][:], own1[:, n : n + 1], 0.0, ALU.add, ALU.is_ge)
+
+        def square(n):
+            inv[n] = keep.tile([P, V], F32, name="inv%d" % n)
+            nc.scalar.activation(out=inv[n][:], in_=root[n][:], func=ACT.Square)
+
+        def signed_mass(n):
+            smass[n] = keep.tile([P, V], F32, name="smass%d" % n)
+            if n < SCALAR_SIGNS:
+                nc.vector.tensor_tensor(smass[n][:], sgn[n][:], mass_t[:], ALU.mult)
+            else:
+                nc.vector.scalar_tensor_tensor(smass[n][:], sgn[n][:], 0.5, mass_t[:], ALU.subtract, ALU.mult)
+
+        def weight(n):
+            gg[n] = keep.tile([P, V], F32, name="gg%d" % n)
+            total[n] = keep.tile([P, 1], F32, name="total%d" % n)
+            nc.vector.scalar_tensor_tensor(
+                gg[n][:], inv[n][:], 1.0, smass[n][:], ALU.mult, ALU.mult, accum_out=total[n][:]
+            )
+
+        def invert_total(n):
+            rtotal[n] = keep.tile([P, 1], F32, name="rtotal%d" % n)
+            nc.vector.reciprocal(rtotal[n][:], total[n][:])
+
+        def normalise(n):
             if n < 2:
-                res = reuse.tile([P, V], F32, name="res%d" % n, align_bytes=64, offset=9216 + 1024 * n)
+                res = reuse.tile([P, V], F32, name="res%d" % n, align_bytes=64, offset=8192 + 1024 * n)
             else:
                 res = keep.tile([P, V], F32, name="res%d" % n)
-            if n < 3:
-                nc.scalar.activation(out=res[:], in_=gg[:], func=ACT.Copy, scale=rtotal[:])
+            if n < SCALAR_SCALINGS:
+                nc.scalar.activation(out=res[:], in_=gg[n][:], func=ACT.Copy, scale=rtotal[n][:])
             else:
-                nc.vector.tensor_scalar(res[:], gg[:], rtotal[:], None, ALU.mult)
+                nc.vector.tensor_scalar(res[:], gg[n][:], rtotal[n][:], None, ALU.mult)
             nc.sync.dma_start(out=out[n * P : (n + 1) * P, :], in_=res[:])
+
+        for n in range(TILES - 1):
+            inverse_root(n)
+            sign(n)
+            if n == TILES - 2:
+                inverse_root(n + 1)
+            square(n)
+        square(TILES - 1)
+        signed_mass(0)
+        sign(3)
+        signed_mass(1)
+        weight(0)
+        signed_mass(3)
+        signed_mass(2)
+        for n in range(1, TILES):
+            weight(n)
+            invert_total(n - 1)
+        invert_total(TILES - 1)
+        for n in range(TILES):
+            normalise(n)

@@ -19,8 +19,7 @@ TILES = S // P
 HALF = H // 2
 GROUPS = HALF // PACK
 BANK = 2048
-SCALAR_GROUPS = 20
-SCALAR_SIGNS = 3
+VECTOR_SIGNS = 2
 SCALAR_SCALINGS = 3
 
 FLOPS = 2 * K * H * S + 2 * H * S * V
@@ -43,7 +42,7 @@ def tile_picked_ydec_as_p_kernel(
         offs_t = keep.tile([P, S // 16], U16, name="offs_t")
         cen_t = keep.tile([P, V // 16], U16, name="cen_t")
         x_tab = keep.tile([P, T], I32, name="x_tab")
-        x_plane = keep.tile([P, T], U8, name="x_plane")
+        x_plane = reuse.tile([P, T], U8, name="x_plane", align_bytes=64, offset=12288)
         e_plane = keep.tile([P, W], U8, name="e_plane")
         e_tab = reuse.tile([P, W], I32, name="e_tab", align_bytes=64, offset=0)
         qn_tab = keep.tile([P, W], F32, name="qn_tab", align_bytes=64)
@@ -57,10 +56,10 @@ def tile_picked_ydec_as_p_kernel(
         nc.vector.memset(warm_in[:], 1.0)
         nc.vector.memset(e_plane[:].bitcast(I32), 0)
         w_rows = w1.rearrange("(p j) c -> p j c", j=PACK)
+        nc.scalar.activation(out=warm_out[:], in_=warm_in[:], func=ACT.Abs_reciprocal_sqrt)
         nc.sync.dma_start(out=w_raw[0][:], in_=w_rows[:, :, 0:HALF])
         nc.sync.dma_start(offs_t[:], offs)
-        load_scales(nc.scalar, x_plane, x_scales)
-        nc.scalar.activation(out=warm_out[:], in_=warm_in[:], func=ACT.Abs_reciprocal_sqrt)
+        load_scales(nc.sync, x_plane, x_scales)
         nc.sync.dma_start(out=w_raw[1][:], in_=w_rows[:, :, HALF:H])
         nc.sync.dma_start(out=x_tab[:], in_=x_words[0].rearrange("p n t -> p (n t)").bitcast(I32))
         nc.sync.dma_start(out=e_tab[:], in_=e_words[0].rearrange("p n t -> p (n t)").bitcast(I32))
@@ -75,14 +74,15 @@ def tile_picked_ydec_as_p_kernel(
         nc.vector.tensor_copy(x_sc[:], x_plane[:].indirect(offs_t[:]))
 
         w_codes = [keep.tile([P, P], U32, name="w_codes%d" % t, align_bytes=64) for t in range(PACK)]
-        w_sc = [keep.tile([P, P], U8, name="w_sc%d" % t, align_bytes=64) for t in range(PACK)]
+        w_sc = [reuse.tile([P, P], U8, name="w_sc%d" % t, align_bytes=64, offset=12288 + P * t) for t in range(PACK)]
         w_bf = [keep.tile([P, PACK, GROUPS, PACK], BF16, name="w_bf%d" % i, align_bytes=64) for i in range(2)]
-        w_dst = [w_bf[i][:].rearrange("p t m j -> p m j t") for i in range(2)]
-        w_src = [w_raw[i][:].rearrange("p j (m t) -> p m j t", t=PACK) for i in range(2)]
-        nc.scalar.copy(out=w_dst[0], in_=w_src[0])
-        nc.scalar.copy(out=w_dst[1][:, 0:SCALAR_GROUPS], in_=w_src[1][:, 0:SCALAR_GROUPS])
-        nc.vector.tensor_copy(out=w_dst[1][:, SCALAR_GROUPS:GROUPS], in_=w_src[1][:, SCALAR_GROUPS:GROUPS])
         for i in range(2):
+            nc.scalar.copy(
+                out=w_bf[i][:].rearrange("p t m j -> p m j t"),
+                in_=w_raw[i][:].rearrange("p j (m t) -> p m j t", t=PACK),
+            )
+
+        def quantise_half(i):
             cols = slice(i * GROUPS, (i + 1) * GROUPS)
             for t in range(PACK):
                 nc.vector.quantize_mx(
@@ -92,10 +92,16 @@ def tile_picked_ydec_as_p_kernel(
                 )
 
         x_codes = []
-        for first, count in ((0, 1), (1, 1), (2, 2)):
+
+        def pick_words(first, count):
             picked = keep.tile([P, count * P], U32, name="x_codes%d" % first, align_bytes=64)
             nc.vector.tensor_copy(picked[:], x_tab[:].bitcast(U32).indirect(offs_t[:, 8 * first : 8 * (first + count)]))
             x_codes.extend(picked[:, i * P : (i + 1) * P] for i in range(count))
+
+        quantise_half(0)
+        pick_words(0, 2)
+        quantise_half(1)
+        pick_words(2, 2)
 
         e_codes = keep.tile([P, V], U32, name="e_codes", align_bytes=64)
         e_sc = keep.tile([P, V], U8, name="e_sc", align_bytes=64)
@@ -115,8 +121,8 @@ def tile_picked_ydec_as_p_kernel(
                     start=True,
                     stop=True,
                 )
-            if n == 1:
-                hb = reuse.tile([P, P, PACK], BF16, name="h_bf%d" % n, align_bytes=64, offset=6144)
+            if n in (1, 2):
+                hb = reuse.tile([P, P, PACK], BF16, name="h_bf%d" % n, align_bytes=64, offset=5120 + 1024 * n)
             else:
                 hb = keep.tile([P, P, PACK], BF16, name="h_bf%d" % n, align_bytes=64)
             nc.scalar.copy(
@@ -130,7 +136,7 @@ def tile_picked_ydec_as_p_kernel(
 
         def second_product(n):
             h_codes = keep.tile([P, P], U32, name="h_codes%d" % n, align_bytes=64)
-            h_sc = reuse.tile([P, P], U8, name="h_sc%d" % n, align_bytes=64, offset=(0, 4096, 6144, 6144 + 128)[n])
+            h_sc = reuse.tile([P, P], U8, name="h_sc%d" % n, align_bytes=64, offset=(0, 4096, 6144, 7168)[n])
             nc.vector.quantize_mx(
                 out=h_codes[:].bitcast(FP8X4), scales=h_sc[:], in_=h_bf[n][:].rearrange("p n t -> p (n t)")
             )
@@ -160,11 +166,6 @@ def tile_picked_ydec_as_p_kernel(
         q_cen = keep.tile([P, V], F32, name="q_cen", align_bytes=64)
         nc.vector.tensor_copy(q_cen[:], qn_tab[:].indirect(cen_t[:]))
         second_product(1)
-        denominator(0)
-        second_product(2)
-        second_product(3)
-        for n in range(1, TILES):
-            denominator(n)
 
         root, inv, sgn, smass, gg, total, rtotal = {}, {}, {}, {}, {}, {}, {}
 
@@ -177,7 +178,7 @@ def tile_picked_ydec_as_p_kernel(
 
         def sign(n):
             sgn[n] = keep.tile([P, V], F32, name="sgn%d" % n)
-            if n < SCALAR_SIGNS:
+            if n >= VECTOR_SIGNS:
                 nc.scalar.activation(out=sgn[n][:], in_=den[n][:], func=ACT.Sign, bias=own1[:, n : n + 1])
             else:
                 nc.vector.tensor_scalar(sgn[n][:], den[n][:], own1[:, n : n + 1], 0.0, ALU.add, ALU.is_ge)
@@ -188,7 +189,7 @@ def tile_picked_ydec_as_p_kernel(
 
         def signed_mass(n):
             smass[n] = keep.tile([P, V], F32, name="smass%d" % n)
-            if n < SCALAR_SIGNS:
+            if n >= VECTOR_SIGNS:
                 nc.vector.tensor_tensor(smass[n][:], sgn[n][:], mass_t[:], ALU.mult)
             else:
                 nc.vector.scalar_tensor_tensor(smass[n][:], sgn[n][:], 0.5, mass_t[:], ALU.subtract, ALU.mult)
@@ -215,22 +216,37 @@ def tile_picked_ydec_as_p_kernel(
                 nc.vector.tensor_scalar(res[:], gg[n][:], rtotal[n][:], None, ALU.mult)
             nc.sync.dma_start(out=out[n * P : (n + 1) * P, :], in_=res[:])
 
-        for n in range(TILES - 1):
-            inverse_root(n)
-            sign(n)
-            if n == TILES - 2:
-                inverse_root(n + 1)
-            square(n)
-        square(TILES - 1)
+        denominator(0)
+        second_product(2)
+        sign(0)
+        denominator(1)
+        second_product(3)
+        sign(1)
+        denominator(2)
         signed_mass(0)
+        denominator(3)
+        inverse_root(0)
+        square(0)
+        inverse_root(1)
+        inverse_root(2)
+        square(1)
+        sign(2)
+        inverse_root(3)
         sign(3)
-        signed_mass(1)
+        square(2)
+        square(3)
         weight(0)
-        signed_mass(3)
+        signed_mass(1)
         signed_mass(2)
-        for n in range(1, TILES):
-            weight(n)
-            invert_total(n - 1)
-        invert_total(TILES - 1)
-        for n in range(TILES):
-            normalise(n)
+        weight(1)
+        invert_total(0)
+        signed_mass(3)
+        weight(2)
+        invert_total(1)
+        weight(3)
+        invert_total(2)
+        invert_total(3)
+        normalise(0)
+        normalise(1)
+        normalise(2)
+        normalise(3)

@@ -19,7 +19,9 @@ TILES = S // P
 HALF = H // 2
 GROUPS = HALF // PACK
 BANK = 2048
-VECTOR_SIGNS = 2
+EARLY = 240
+SCALAR_GROUPS = 30
+VECTOR_SIGNS = 1
 SCALAR_SCALINGS = 3
 
 FLOPS = 2 * K * H * S + 2 * H * S * V
@@ -42,13 +44,13 @@ def tile_picked_ydec_as_p_kernel(
         offs_t = keep.tile([P, S // 16], U16, name="offs_t")
         cen_t = keep.tile([P, V // 16], U16, name="cen_t")
         x_tab = keep.tile([P, T], I32, name="x_tab")
-        x_plane = reuse.tile([P, T], U8, name="x_plane", align_bytes=64, offset=12288)
+        x_plane = keep.tile([P, T], U8, name="x_plane")
         e_plane = keep.tile([P, W], U8, name="e_plane")
         e_tab = reuse.tile([P, W], I32, name="e_tab", align_bytes=64, offset=0)
         qn_tab = keep.tile([P, W], F32, name="qn_tab", align_bytes=64)
         mass_t = keep.tile([P, V], F32, name="mass_t")
         own_t = reuse.tile([P, 64], F32, name="own_t", align_bytes=64, offset=4096)
-        w_raw = [keep.tile([P, PACK, HALF], F32, name="w_raw%d" % i) for i in range(2)]
+        w_raw = [keep.tile([P, PACK, width], F32, name="w_raw%d" % width) for width in (EARLY, H - EARLY)]
 
         nc.vector.memset(x_plane[:].bitcast(I32), 0)
         warm_in = keep.tile([P, 1], F32, name="warm_in")
@@ -57,10 +59,10 @@ def tile_picked_ydec_as_p_kernel(
         nc.vector.memset(e_plane[:].bitcast(I32), 0)
         w_rows = w1.rearrange("(p j) c -> p j c", j=PACK)
         nc.scalar.activation(out=warm_out[:], in_=warm_in[:], func=ACT.Abs_reciprocal_sqrt)
-        nc.sync.dma_start(out=w_raw[0][:], in_=w_rows[:, :, 0:HALF])
+        nc.sync.dma_start(out=w_raw[0][:], in_=w_rows[:, :, 0:EARLY])
         nc.sync.dma_start(offs_t[:], offs)
         load_scales(nc.sync, x_plane, x_scales)
-        nc.sync.dma_start(out=w_raw[1][:], in_=w_rows[:, :, HALF:H])
+        nc.sync.dma_start(out=w_raw[1][:], in_=w_rows[:, :, EARLY:H])
         nc.sync.dma_start(out=x_tab[:], in_=x_words[0].rearrange("p n t -> p (n t)").bitcast(I32))
         nc.sync.dma_start(out=e_tab[:], in_=e_words[0].rearrange("p n t -> p (n t)").bitcast(I32))
         load_scales(nc.sync, e_plane, e_scales)
@@ -74,13 +76,15 @@ def tile_picked_ydec_as_p_kernel(
         nc.vector.tensor_copy(x_sc[:], x_plane[:].indirect(offs_t[:]))
 
         w_codes = [keep.tile([P, P], U32, name="w_codes%d" % t, align_bytes=64) for t in range(PACK)]
-        w_sc = [reuse.tile([P, P], U8, name="w_sc%d" % t, align_bytes=64, offset=12288 + P * t) for t in range(PACK)]
+        w_sc = [keep.tile([P, P], U8, name="w_sc%d" % t, align_bytes=64) for t in range(PACK)]
         w_bf = [keep.tile([P, PACK, GROUPS, PACK], BF16, name="w_bf%d" % i, align_bytes=64) for i in range(2)]
-        for i in range(2):
-            nc.scalar.copy(
-                out=w_bf[i][:].rearrange("p t m j -> p m j t"),
-                in_=w_raw[i][:].rearrange("p j (m t) -> p m j t", t=PACK),
-            )
+        w_dst = [w_bf[i][:].rearrange("p t m j -> p m j t") for i in range(2)]
+        w_src = [w_raw[i][:].rearrange("p j (m t) -> p m j t", t=PACK) for i in range(2)]
+        rest = GROUPS - EARLY // PACK
+        nc.scalar.copy(out=w_dst[0][:, 0 : GROUPS - rest], in_=w_src[0])
+        nc.scalar.copy(out=w_dst[0][:, GROUPS - rest : GROUPS], in_=w_src[1][:, 0:rest])
+        nc.scalar.copy(out=w_dst[1][:, 0:SCALAR_GROUPS], in_=w_src[1][:, rest : rest + SCALAR_GROUPS])
+        nc.vector.tensor_copy(out=w_dst[1][:, SCALAR_GROUPS:GROUPS], in_=w_src[1][:, rest + SCALAR_GROUPS : rest + GROUPS])
 
         def quantise_half(i):
             cols = slice(i * GROUPS, (i + 1) * GROUPS)
@@ -99,8 +103,9 @@ def tile_picked_ydec_as_p_kernel(
             x_codes.extend(picked[:, i * P : (i + 1) * P] for i in range(count))
 
         quantise_half(0)
-        pick_words(0, 2)
         quantise_half(1)
+        pick_words(0, 1)
+        pick_words(1, 1)
         pick_words(2, 2)
 
         e_codes = keep.tile([P, V], U32, name="e_codes", align_bytes=64)
@@ -219,17 +224,17 @@ def tile_picked_ydec_as_p_kernel(
         denominator(0)
         second_product(2)
         sign(0)
-        denominator(1)
         second_product(3)
-        sign(1)
+        denominator(1)
         denominator(2)
         signed_mass(0)
         denominator(3)
         inverse_root(0)
         square(0)
         inverse_root(1)
-        inverse_root(2)
+        sign(1)
         square(1)
+        inverse_root(2)
         sign(2)
         inverse_root(3)
         sign(3)

@@ -19,7 +19,7 @@ TILES = S // P
 HALF = H // 2
 GROUPS = HALF // PACK
 BANK = 2048
-EARLY = 240
+SEAM = 2
 SCALAR_GROUPS = 30
 VECTOR_SIGNS = 1
 SCALAR_SCALINGS = 3
@@ -50,7 +50,7 @@ def tile_picked_ydec_as_p_kernel(
         qn_tab = keep.tile([P, W], F32, name="qn_tab", align_bytes=64)
         mass_t = keep.tile([P, V], F32, name="mass_t")
         own_t = reuse.tile([P, 64], F32, name="own_t", align_bytes=64, offset=4096)
-        w_raw = [keep.tile([P, PACK, width], F32, name="w_raw%d" % width) for width in (EARLY, H - EARLY)]
+        w_raw = keep.tile([P, PACK, H], F32, name="w_raw")
 
         nc.vector.memset(x_plane[:].bitcast(I32), 0)
         warm_in = keep.tile([P, 1], F32, name="warm_in")
@@ -59,10 +59,10 @@ def tile_picked_ydec_as_p_kernel(
         nc.vector.memset(e_plane[:].bitcast(I32), 0)
         w_rows = w1.rearrange("(p j) c -> p j c", j=PACK)
         nc.scalar.activation(out=warm_out[:], in_=warm_in[:], func=ACT.Abs_reciprocal_sqrt)
-        nc.sync.dma_start(out=w_raw[0][:], in_=w_rows[:, :, 0:EARLY])
+        nc.sync.dma_start(out=w_raw[:, :, 0:HALF], in_=w_rows[:, :, 0:HALF])
         nc.sync.dma_start(offs_t[:], offs)
         load_scales(nc.sync, x_plane, x_scales)
-        nc.sync.dma_start(out=w_raw[1][:], in_=w_rows[:, :, EARLY:H])
+        nc.sync.dma_start(out=w_raw[:, :, HALF:H], in_=w_rows[:, :, HALF:H])
         nc.sync.dma_start(out=x_tab[:], in_=x_words[0].rearrange("p n t -> p (n t)").bitcast(I32))
         nc.sync.dma_start(out=e_tab[:], in_=e_words[0].rearrange("p n t -> p (n t)").bitcast(I32))
         load_scales(nc.sync, e_plane, e_scales)
@@ -77,14 +77,13 @@ def tile_picked_ydec_as_p_kernel(
 
         w_codes = [keep.tile([P, P], U32, name="w_codes%d" % t, align_bytes=64) for t in range(PACK)]
         w_sc = [keep.tile([P, P], U8, name="w_sc%d" % t, align_bytes=64) for t in range(PACK)]
-        w_bf = [keep.tile([P, PACK, GROUPS, PACK], BF16, name="w_bf%d" % i, align_bytes=64) for i in range(2)]
-        w_dst = [w_bf[i][:].rearrange("p t m j -> p m j t") for i in range(2)]
-        w_src = [w_raw[i][:].rearrange("p j (m t) -> p m j t", t=PACK) for i in range(2)]
-        rest = GROUPS - EARLY // PACK
-        nc.scalar.copy(out=w_dst[0][:, 0 : GROUPS - rest], in_=w_src[0])
-        nc.scalar.copy(out=w_dst[0][:, GROUPS - rest : GROUPS], in_=w_src[1][:, 0:rest])
-        nc.scalar.copy(out=w_dst[1][:, 0:SCALAR_GROUPS], in_=w_src[1][:, rest : rest + SCALAR_GROUPS])
-        nc.vector.tensor_copy(out=w_dst[1][:, SCALAR_GROUPS:GROUPS], in_=w_src[1][:, rest + SCALAR_GROUPS : rest + GROUPS])
+        w_bf = keep.tile([P, PACK, P, PACK], BF16, name="w_bf", align_bytes=64)
+        w_dst = w_bf[:].rearrange("p t m j -> p m j t")
+        w_src = w_raw[:].rearrange("p j (m t) -> p m j t", t=PACK)
+        cuts = (0, GROUPS - SEAM, GROUPS + SEAM, GROUPS + SCALAR_GROUPS)
+        for lo, hi in zip(cuts, cuts[1:]):
+            nc.scalar.copy(out=w_dst[:, lo:hi], in_=w_src[:, lo:hi])
+        nc.vector.tensor_copy(out=w_dst[:, cuts[-1] : P], in_=w_src[:, cuts[-1] : P])
 
         def quantise_half(i):
             cols = slice(i * GROUPS, (i + 1) * GROUPS)
@@ -92,7 +91,7 @@ def tile_picked_ydec_as_p_kernel(
                 nc.vector.quantize_mx(
                     out=w_codes[t][:, cols].bitcast(FP8X4),
                     scales=w_sc[t][:, cols],
-                    in_=w_bf[i][:, t].rearrange("p m j -> p (m j)"),
+                    in_=w_bf[:, t, cols].rearrange("p m j -> p (m j)"),
                 )
 
         x_codes = []

@@ -22,7 +22,7 @@ BANK = 2048
 SEAM = 2
 SCALAR_GROUPS = 30
 VECTOR_SIGNS = 1
-SCALAR_SCALINGS = 3
+SCALAR_SCALINGS = 2
 
 FLOPS = 2 * K * H * S + 2 * H * S * V
 
@@ -171,7 +171,9 @@ def tile_picked_ydec_as_p_kernel(
         nc.vector.tensor_copy(q_cen[:], qn_tab[:].indirect(cen_t[:]))
         second_product(1)
 
-        root, inv, sgn, smass, gg, total, rtotal = {}, {}, {}, {}, {}, {}, {}
+        root, inv, sgn, smass, gg = {}, {}, {}, {}, {}
+        total = keep.tile([P, TILES], F32, name="total")
+        rtotal = keep.tile([P, TILES], F32, name="rtotal")
 
         def inverse_root(n):
             if n == TILES - 1:
@@ -200,14 +202,12 @@ def tile_picked_ydec_as_p_kernel(
 
         def weight(n):
             gg[n] = keep.tile([P, V], F32, name="gg%d" % n)
-            total[n] = keep.tile([P, 1], F32, name="total%d" % n)
             nc.vector.scalar_tensor_tensor(
-                gg[n][:], inv[n][:], 1.0, smass[n][:], ALU.mult, ALU.mult, accum_out=total[n][:]
+                gg[n][:], inv[n][:], 1.0, smass[n][:], ALU.mult, ALU.mult, accum_out=total[:, n : n + 1]
             )
 
-        def invert_total(n):
-            rtotal[n] = keep.tile([P, 1], F32, name="rtotal%d" % n)
-            nc.vector.reciprocal(rtotal[n][:], total[n][:])
+        def invert_total(first, last):
+            nc.vector.reciprocal(rtotal[:, first : last + 1], total[:, first : last + 1])
 
         def normalise(n):
             if n < 2:
@@ -215,9 +215,9 @@ def tile_picked_ydec_as_p_kernel(
             else:
                 res = keep.tile([P, V], F32, name="res%d" % n)
             if n < SCALAR_SCALINGS:
-                nc.scalar.activation(out=res[:], in_=gg[n][:], func=ACT.Copy, scale=rtotal[n][:])
+                nc.scalar.activation(out=res[:], in_=gg[n][:], func=ACT.Copy, scale=rtotal[:, n : n + 1])
             else:
-                nc.vector.tensor_scalar(res[:], gg[n][:], rtotal[n][:], None, ALU.mult)
+                nc.vector.tensor_scalar(res[:], gg[n][:], rtotal[:, n : n + 1], None, ALU.mult)
             nc.sync.dma_start(out=out[n * P : (n + 1) * P, :], in_=res[:])
 
         denominator(0)
@@ -243,13 +243,12 @@ def tile_picked_ydec_as_p_kernel(
         signed_mass(1)
         signed_mass(2)
         weight(1)
-        invert_total(0)
         signed_mass(3)
+        invert_total(0, 1)
         weight(2)
-        invert_total(1)
         weight(3)
-        invert_total(2)
-        invert_total(3)
+        invert_total(2, 2)
+        invert_total(3, 3)
         normalise(0)
         normalise(1)
         normalise(2)

@@ -21,8 +21,8 @@ GROUPS = HALF // PACK
 BANK = 2048
 SEAM = 2
 SCALAR_GROUPS = 30
-VECTOR_SIGNS = 1
-SCALAR_SCALINGS = 2
+SCALAR_SIGNS = 2
+SCALAR_SCALINGS = 1
 
 FLOPS = 2 * K * H * S + 2 * H * S * V
 
@@ -125,7 +125,7 @@ def tile_picked_ydec_as_p_kernel(
                     start=True,
                     stop=True,
                 )
-            if n in (1, 2):
+            if n == 1:
                 hb = reuse.tile([P, P, PACK], BF16, name="h_bf%d" % n, align_bytes=64, offset=5120 + 1024 * n)
             else:
                 hb = keep.tile([P, P, PACK], BF16, name="h_bf%d" % n, align_bytes=64)
@@ -140,7 +140,7 @@ def tile_picked_ydec_as_p_kernel(
 
         def second_product(n):
             h_codes = keep.tile([P, P], U32, name="h_codes%d" % n, align_bytes=64)
-            h_sc = reuse.tile([P, P], U8, name="h_sc%d" % n, align_bytes=64, offset=(0, 4096, 6144, 7168)[n])
+            h_sc = reuse.tile([P, P], U8, name="h_sc%d" % n, align_bytes=64, offset=(0, 4096, 6144, 6144 + 128)[n])
             nc.vector.quantize_mx(
                 out=h_codes[:].bitcast(FP8X4), scales=h_sc[:], in_=h_bf[n][:].rearrange("p n t -> p (n t)")
             )
@@ -176,15 +176,17 @@ def tile_picked_ydec_as_p_kernel(
         rtotal = keep.tile([P, TILES], F32, name="rtotal")
 
         def inverse_root(n):
-            if n == TILES - 1:
-                root[n] = reuse.tile([P, V], F32, name="root%d" % n, align_bytes=64, offset=8192 + 512)
+            if n == 2:
+                root[n] = reuse.tile([P, V], F32, name="root%d" % n, align_bytes=64, offset=8192 + 1024 * (n - 2))
+            elif n == 1:
+                root[n] = reuse.tile([P, V], F32, name="root%d" % n, align_bytes=64, offset=4096 + 128)
             else:
                 root[n] = keep.tile([P, V], F32, name="root%d" % n)
             nc.scalar.activation(out=root[n][:], in_=den[n][:], func=ACT.Abs_reciprocal_sqrt, bias=own1[:, n : n + 1])
 
         def sign(n):
             sgn[n] = keep.tile([P, V], F32, name="sgn%d" % n)
-            if n >= VECTOR_SIGNS:
+            if n < SCALAR_SIGNS:
                 nc.scalar.activation(out=sgn[n][:], in_=den[n][:], func=ACT.Sign, bias=own1[:, n : n + 1])
             else:
                 nc.vector.tensor_scalar(sgn[n][:], den[n][:], own1[:, n : n + 1], 0.0, ALU.add, ALU.is_ge)
@@ -195,7 +197,7 @@ def tile_picked_ydec_as_p_kernel(
 
         def signed_mass(n):
             smass[n] = keep.tile([P, V], F32, name="smass%d" % n)
-            if n >= VECTOR_SIGNS:
+            if n < SCALAR_SIGNS:
                 nc.vector.tensor_tensor(smass[n][:], sgn[n][:], mass_t[:], ALU.mult)
             else:
                 nc.vector.scalar_tensor_tensor(smass[n][:], sgn[n][:], 0.5, mass_t[:], ALU.subtract, ALU.mult)
@@ -210,7 +212,7 @@ def tile_picked_ydec_as_p_kernel(
             nc.vector.reciprocal(rtotal[:, first : last + 1], total[:, first : last + 1])
 
         def normalise(n):
-            if n < 2:
+            if n < SCALAR_SCALINGS:
                 res = reuse.tile([P, V], F32, name="res%d" % n, align_bytes=64, offset=8192 + 1024 * n)
             else:
                 res = keep.tile([P, V], F32, name="res%d" % n)
@@ -222,34 +224,35 @@ def tile_picked_ydec_as_p_kernel(
 
         denominator(0)
         second_product(2)
-        sign(0)
         second_product(3)
         denominator(1)
         denominator(2)
-        signed_mass(0)
         denominator(3)
         inverse_root(0)
+        sign(0)
         square(0)
         inverse_root(1)
         sign(1)
         square(1)
         inverse_root(2)
-        sign(2)
         inverse_root(3)
-        sign(3)
         square(2)
         square(3)
+        signed_mass(0)
+        sign(2)
+        sign(3)
         weight(0)
         signed_mass(1)
         signed_mass(2)
+        invert_total(0, 0)
         weight(1)
         signed_mass(3)
-        invert_total(0, 1)
+        invert_total(1, 1)
         weight(2)
         weight(3)
         invert_total(2, 2)
-        invert_total(3, 3)
         normalise(0)
         normalise(1)
+        invert_total(3, 3)
         normalise(2)
         normalise(3)

@@ -163,12 +163,14 @@ def tile_picked_ydec_as_p_kernel(
                 d = reuse.tile([P, V], F32, name="den%d" % n, align_bytes=64, offset=4096 + 128)
             else:
                 d = keep.tile([P, V], F32, name="den%d" % n)
-            nc.vector.scalar_tensor_tensor(d[:], y_ps[n][:], -0.2, q_cen[:], ALU.mult, ALU.add)
+            for cols in (slice(0, P), slice(P, V)) if n == 0 else (slice(0, V),):
+                nc.vector.scalar_tensor_tensor(d[:, cols], y_ps[n][:, cols], -0.2, q_cen[:, cols], ALU.mult, ALU.add)
             den.append(d)
 
         second_product(0)
         q_cen = keep.tile([P, V], F32, name="q_cen", align_bytes=64)
-        nc.vector.tensor_copy(q_cen[:], qn_tab[:].indirect(cen_t[:]))
+        for i in range(2):
+            nc.vector.tensor_copy(q_cen[:, i * P : (i + 1) * P], qn_tab[:].indirect(cen_t[:, 8 * i : 8 * (i + 1)]))
         second_product(1)
 
         root, inv, sgn, smass, gg = {}, {}, {}, {}, {}
@@ -233,8 +235,8 @@ def tile_picked_ydec_as_p_kernel(
         square(0)
         inverse_root(1)
         sign(1)
-        square(1)
         inverse_root(2)
+        square(1)
         inverse_root(3)
         square(2)
         square(3)
@@ -247,8 +249,8 @@ def tile_picked_ydec_as_p_kernel(
         invert_total(0, 0)
         weight(1)
         signed_mass(3)
-        invert_total(1, 1)
         weight(2)
+        invert_total(1, 1)
         weight(3)
         invert_total(2, 2)
         normalise(0)

@@ -21,8 +21,9 @@ GROUPS = HALF // PACK
 BANK = 2048
 SEAM = 2
 SCALAR_GROUPS = 30
-SCALAR_SIGNS = 2
-SCALAR_SCALINGS = 1
+SCALAR_SCALINGS = 2
+ROOTS = 8192
+SIGN_BIT = -(2**31)
 
 FLOPS = 2 * K * H * S + 2 * H * S * V
 
@@ -49,7 +50,8 @@ def tile_picked_ydec_as_p_kernel(
         e_tab = reuse.tile([P, W], I32, name="e_tab", align_bytes=64, offset=0)
         qn_tab = keep.tile([P, W], F32, name="qn_tab", align_bytes=64)
         mass_t = keep.tile([P, V], F32, name="mass_t")
-        own_t = reuse.tile([P, 64], F32, name="own_t", align_bytes=64, offset=4096)
+        own_t = reuse.tile([P, 512], F32, name="own_t", align_bytes=64, offset=4096)
+        five = keep.tile([P, P], F32, name="five")
         w_raw = keep.tile([P, PACK, H], F32, name="w_raw")
 
         nc.vector.memset(x_plane[:].bitcast(I32), 0)
@@ -57,6 +59,7 @@ def tile_picked_ydec_as_p_kernel(
         warm_out = keep.tile([P, 1], F32, name="warm_out")
         nc.vector.memset(warm_in[:], 1.0)
         nc.vector.memset(e_plane[:].bitcast(I32), 0)
+        nc.vector.memset(five[:], 5.0)
         w_rows = w1.rearrange("(p j) c -> p j c", j=PACK)
         nc.scalar.activation(out=warm_out[:], in_=warm_in[:], func=ACT.Abs_reciprocal_sqrt)
         nc.sync.dma_start(out=w_raw[:, :, 0:HALF], in_=w_rows[:, :, 0:HALF])
@@ -112,12 +115,13 @@ def tile_picked_ydec_as_p_kernel(
         nc.vector.tensor_copy(e_codes[:], e_tab[:].bitcast(U32).indirect(cen_t[:]))
         nc.vector.tensor_copy(e_sc[:], e_plane[:].indirect(cen_t[:]))
 
-        h_bf = []
-        for n in range(TILES):
-            h_ps = psum.tile([P, PACK, P], F32, name="h_ps%d" % n, offset=n * BANK)
+        h_ps, h_bf = {}, {}
+
+        def first_product(n):
+            h_ps[n] = psum.tile([P, PACK, P], F32, name="h_ps%d" % n, offset=n * BANK)
             for t in range(PACK):
                 nc.tensor.matmul_mx(
-                    out=h_ps[:, t, :],
+                    out=h_ps[n][:, t, :],
                     lhsT=w_codes[t][:].bitcast(FP8X4),
                     lhsT_scale=w_sc[t][:],
                     rhs=x_codes[n].bitcast(FP8X4),
@@ -125,28 +129,28 @@ def tile_picked_ydec_as_p_kernel(
                     start=True,
                     stop=True,
                 )
-            if n == 1:
-                hb = reuse.tile([P, P, PACK], BF16, name="h_bf%d" % n, align_bytes=64, offset=5120 + 1024 * n)
-            else:
-                hb = keep.tile([P, P, PACK], BF16, name="h_bf%d" % n, align_bytes=64)
-            nc.scalar.copy(
-                out=hb[:].rearrange("p (c i) t -> p c t i", i=2), in_=h_ps[:].rearrange("p t (c i) -> p c t i", i=2)
-            )
-            h_bf.append(hb)
-        own1 = keep.tile([P, TILES], F32, name="own1")
-        nc.gpsimd.tensor_scalar(own1[:], own_t[:, 0:TILES], 1.0, 1.0, ALU.mult, ALU.add)
 
-        y_ps = []
+        def round_h(n):
+            if n % 2 == 1:
+                h_bf[n] = reuse.tile([P, P, PACK], BF16, name="h_bf%d" % n, align_bytes=64, offset={1: 6144, 3: 5120}[n])
+            else:
+                h_bf[n] = keep.tile([P, P, PACK], BF16, name="h_bf%d" % n, align_bytes=64)
+            nc.scalar.copy(
+                out=h_bf[n][:].rearrange("p (c i) t -> p c t i", i=2),
+                in_=h_ps[n][:].rearrange("p t (c i) -> p c t i", i=2),
+            )
+
+        y_ps = {}
 
         def second_product(n):
             h_codes = keep.tile([P, P], U32, name="h_codes%d" % n, align_bytes=64)
-            h_sc = reuse.tile([P, P], U8, name="h_sc%d" % n, align_bytes=64, offset=(0, 4096, 6144, 6144 + 128)[n])
+            h_sc = reuse.tile([P, P], U8, name="h_sc%d" % n, align_bytes=64, offset=(0, 4096, 6144, 128)[n])
             nc.vector.quantize_mx(
                 out=h_codes[:].bitcast(FP8X4), scales=h_sc[:], in_=h_bf[n][:].rearrange("p n t -> p (n t)")
             )
-            y = psum.tile([P, V], F32, name="y_ps%d" % n, offset=(TILES + n) * BANK)
+            y_ps[n] = psum.tile([P, V], F32, name="y_ps%d" % n, offset=(TILES + n) * BANK)
             nc.tensor.matmul_mx(
-                out=y[:],
+                out=y_ps[n][:],
                 lhsT=h_codes[:].bitcast(FP8X4),
                 lhsT_scale=h_sc[:],
                 rhs=e_codes[:].bitcast(FP8X4),
@@ -154,55 +158,48 @@ def tile_picked_ydec_as_p_kernel(
                 start=True,
                 stop=True,
             )
-            y_ps.append(y)
 
-        den = []
-
-        def denominator(n):
-            if n == 0:
-                d = reuse.tile([P, V], F32, name="den%d" % n, align_bytes=64, offset=4096 + 128)
-            else:
-                d = keep.tile([P, V], F32, name="den%d" % n)
-            for cols in (slice(0, P), slice(P, V)) if n == 0 else (slice(0, V),):
-                nc.vector.scalar_tensor_tensor(d[:, cols], y_ps[n][:, cols], -0.2, q_cen[:, cols], ALU.mult, ALU.add)
-            den.append(d)
-
-        second_product(0)
-        q_cen = keep.tile([P, V], F32, name="q_cen", align_bytes=64)
-        for i in range(2):
-            nc.vector.tensor_copy(q_cen[:, i * P : (i + 1) * P], qn_tab[:].indirect(cen_t[:, 8 * i : 8 * (i + 1)]))
-        second_product(1)
-
-        root, inv, sgn, smass, gg = {}, {}, {}, {}, {}
+        own5 = keep.tile([P, TILES], F32, name="own5")
+        q5 = keep.tile([P, V], F32, name="q5", align_bytes=64)
+        den, root, inv, smass, gg = {}, {}, {}, {}, {}
         total = keep.tile([P, TILES], F32, name="total")
-        rtotal = keep.tile([P, TILES], F32, name="rtotal")
+        rtotal = {}
+
+        def denominator(n, cols=slice(0, V)):
+            if n not in den:
+                den[n] = keep.tile([P, V], F32, name="den%d" % n)
+            nc.vector.scalar_tensor_tensor(
+                den[n][:, cols], y_ps[n][:, cols], own5[:, n : n + 1], q5[:, cols], ALU.subtract, ALU.subtract
+            )
+
+        def pick_norms(i):
+            picked = qn_tab[:].indirect(cen_t[:, 8 * i : 8 * (i + 1)])
+            if i == 0:
+                nc.vector.tensor_tensor(q5[:, 0:P], picked, five[:], ALU.mult)
+            else:
+                nc.scalar.activation(out=q5[:, P:V], in_=picked, func=ACT.Copy, scale=5.0)
 
         def inverse_root(n):
-            if n == 2:
-                root[n] = reuse.tile([P, V], F32, name="root%d" % n, align_bytes=64, offset=8192 + 1024 * (n - 2))
-            elif n == 1:
-                root[n] = reuse.tile([P, V], F32, name="root%d" % n, align_bytes=64, offset=4096 + 128)
-            else:
-                root[n] = keep.tile([P, V], F32, name="root%d" % n)
-            nc.scalar.activation(out=root[n][:], in_=den[n][:], func=ACT.Abs_reciprocal_sqrt, bias=own1[:, n : n + 1])
-
-        def sign(n):
-            sgn[n] = keep.tile([P, V], F32, name="sgn%d" % n)
-            if n < SCALAR_SIGNS:
-                nc.scalar.activation(out=sgn[n][:], in_=den[n][:], func=ACT.Sign, bias=own1[:, n : n + 1])
-            else:
-                nc.vector.tensor_scalar(sgn[n][:], den[n][:], own1[:, n : n + 1], 0.0, ALU.add, ALU.is_ge)
+            root[n] = reuse.tile([P, V], F32, name="root%d" % n, align_bytes=64, offset=ROOTS + 1024 * n)
+            nc.scalar.activation(out=root[n][:], in_=den[n][:], func=ACT.Abs_reciprocal_sqrt)
 
         def square(n):
             inv[n] = keep.tile([P, V], F32, name="inv%d" % n)
             nc.scalar.activation(out=inv[n][:], in_=root[n][:], func=ACT.Square)
 
         def signed_mass(n):
-            smass[n] = keep.tile([P, V], F32, name="smass%d" % n)
-            if n < SCALAR_SIGNS:
-                nc.vector.tensor_tensor(smass[n][:], sgn[n][:], mass_t[:], ALU.mult)
+            if n >= 2:
+                smass[n] = reuse.tile([P, V], F32, name="smass%d" % n, align_bytes=64, offset=ROOTS + 1024 * (n - 2))
             else:
-                nc.vector.scalar_tensor_tensor(smass[n][:], sgn[n][:], 0.5, mass_t[:], ALU.subtract, ALU.mult)
+                smass[n] = keep.tile([P, V], F32, name="smass%d" % n)
+            nc.vector.scalar_tensor_tensor(
+                smass[n][:].bitcast(I32),
+                den[n][:].bitcast(I32),
+                SIGN_BIT,
+                mass_t[:].bitcast(I32),
+                ALU.bitwise_and,
+                ALU.bitwise_xor,
+            )
 
         def weight(n):
             gg[n] = keep.tile([P, V], F32, name="gg%d" % n)
@@ -210,51 +207,63 @@ def tile_picked_ydec_as_p_kernel(
                 gg[n][:], inv[n][:], 1.0, smass[n][:], ALU.mult, ALU.mult, accum_out=total[:, n : n + 1]
             )
 
-        def invert_total(first, last):
-            nc.vector.reciprocal(rtotal[:, first : last + 1], total[:, first : last + 1])
+        def invert_total(n):
+            if n == 2:
+                rtotal[n] = reuse.tile([P, 1], F32, name="rtotal%d" % n, align_bytes=64, offset=ROOTS + 3072)
+            else:
+                rtotal[n] = keep.tile([P, 1], F32, name="rtotal%d" % n)
+            nc.vector.reciprocal(rtotal[n][:], total[:, n : n + 1])
 
         def normalise(n):
-            if n < SCALAR_SCALINGS:
-                res = reuse.tile([P, V], F32, name="res%d" % n, align_bytes=64, offset=8192 + 1024 * n)
+            if n == 0:
+                res = reuse.tile([P, V], F32, name="res%d" % n, align_bytes=64, offset=ROOTS + 2048)
             else:
                 res = keep.tile([P, V], F32, name="res%d" % n)
             if n < SCALAR_SCALINGS:
-                nc.scalar.activation(out=res[:], in_=gg[n][:], func=ACT.Copy, scale=rtotal[:, n : n + 1])
+                nc.scalar.activation(out=res[:], in_=gg[n][:], func=ACT.Copy, scale=rtotal[n][:])
             else:
-                nc.vector.tensor_scalar(res[:], gg[n][:], rtotal[:, n : n + 1], None, ALU.mult)
+                nc.vector.tensor_scalar(res[:], gg[n][:], rtotal[n][:], None, ALU.mult)
             nc.sync.dma_start(out=out[n * P : (n + 1) * P, :], in_=res[:])
 
-        denominator(0)
+        for n in range(TILES):
+            first_product(n)
+        nc.gpsimd.tensor_scalar(own5[:], own_t[:, 0:TILES], 5.0, 5.0, ALU.mult, ALU.add)
+        round_h(0)
+        round_h(1)
+        round_h(2)
+        second_product(0)
+        pick_norms(0)
+        pick_norms(1)
+        second_product(1)
+        round_h(3)
+        denominator(0, slice(0, P))
         second_product(2)
-        second_product(3)
+        denominator(0, slice(P, V))
         denominator(1)
+        signed_mass(0)
+        second_product(3)
         denominator(2)
+        signed_mass(1)
         denominator(3)
         inverse_root(0)
-        sign(0)
-        square(0)
         inverse_root(1)
-        sign(1)
+        square(0)
         inverse_root(2)
         square(1)
         inverse_root(3)
         square(2)
         square(3)
-        signed_mass(0)
-        sign(2)
-        sign(3)
         weight(0)
-        signed_mass(1)
         signed_mass(2)
-        invert_total(0, 0)
+        invert_total(0)
         weight(1)
         signed_mass(3)
+        invert_total(1)
         weight(2)
-        invert_total(1, 1)
         weight(3)
-        invert_total(2, 2)
+        invert_total(2)
         normalise(0)
         normalise(1)
-        invert_total(3, 3)
+        invert_total(3)
         normalise(2)
         normalise(3)

@@ -50,7 +50,7 @@ def tile_picked_ydec_as_p_kernel(
         e_tab = reuse.tile([P, W], I32, name="e_tab", align_bytes=64, offset=0)
         qn_tab = keep.tile([P, W], F32, name="qn_tab", align_bytes=64)
         mass_t = keep.tile([P, V], F32, name="mass_t")
-        own_t = reuse.tile([P, 512], F32, name="own_t", align_bytes=64, offset=4096)
+        own_t = reuse.tile([P, 64], F32, name="own_t", align_bytes=64, offset=4096)
         five = keep.tile([P, P], F32, name="five")
         w_raw = keep.tile([P, PACK, H], F32, name="w_raw")
 
@@ -131,8 +131,8 @@ def tile_picked_ydec_as_p_kernel(
                 )
 
         def round_h(n):
-            if n % 2 == 1:
-                h_bf[n] = reuse.tile([P, P, PACK], BF16, name="h_bf%d" % n, align_bytes=64, offset={1: 6144, 3: 5120}[n])
+            if n == 1:
+                h_bf[n] = reuse.tile([P, P, PACK], BF16, name="h_bf%d" % n, align_bytes=64, offset=6144)
             else:
                 h_bf[n] = keep.tile([P, P, PACK], BF16, name="h_bf%d" % n, align_bytes=64)
             nc.scalar.copy(
@@ -144,7 +144,7 @@ def tile_picked_ydec_as_p_kernel(
 
         def second_product(n):
             h_codes = keep.tile([P, P], U32, name="h_codes%d" % n, align_bytes=64)
-            h_sc = reuse.tile([P, P], U8, name="h_sc%d" % n, align_bytes=64, offset=(0, 4096, 6144, 128)[n])
+            h_sc = reuse.tile([P, P], U8, name="h_sc%d" % n, align_bytes=64, offset=(0, 4096, 6144, 6144 + 128)[n])
             nc.vector.quantize_mx(
                 out=h_codes[:].bitcast(FP8X4), scales=h_sc[:], in_=h_bf[n][:].rearrange("p n t -> p (n t)")
             )
@@ -174,10 +174,7 @@ def tile_picked_ydec_as_p_kernel(
 
         def pick_norms(i):
             picked = qn_tab[:].indirect(cen_t[:, 8 * i : 8 * (i + 1)])
-            if i == 0:
-                nc.vector.tensor_tensor(q5[:, 0:P], picked, five[:], ALU.mult)
-            else:
-                nc.scalar.activation(out=q5[:, P:V], in_=picked, func=ACT.Copy, scale=5.0)
+            nc.vector.tensor_tensor(q5[:, i * P : (i + 1) * P], picked, five[:], ALU.mult)
 
         def inverse_root(n):
             root[n] = reuse.tile([P, V], F32, name="root%d" % n, align_bytes=64, offset=ROOTS + 1024 * n)
@@ -231,20 +228,20 @@ def tile_picked_ydec_as_p_kernel(
         round_h(0)
         round_h(1)
         round_h(2)
+        round_h(3)
         second_product(0)
         pick_norms(0)
         pick_norms(1)
         second_product(1)
-        round_h(3)
         denominator(0, slice(0, P))
-        second_product(2)
         denominator(0, slice(P, V))
+        second_product(2)
+        second_product(3)
         denominator(1)
         signed_mass(0)
-        second_product(3)
         denominator(2)
-        signed_mass(1)
         denominator(3)
+        signed_mass(1)
         inverse_root(0)
         inverse_root(1)
         square(0)

@@ -213,7 +213,7 @@ def tile_picked_ydec_as_p_kernel(
 
         def normalise(n):
             if n == 0:
-                res = reuse.tile([P, V], F32, name="res%d" % n, align_bytes=64, offset=ROOTS + 2048)
+                res = reuse.tile([P, V], F32, name="res%d" % n, align_bytes=64, offset=ROOTS + 3072 + 64)
             else:
                 res = keep.tile([P, V], F32, name="res%d" % n)
             if n < SCALAR_SCALINGS:

@@ -1,6 +1,7 @@
 from contextlib import ExitStack
 
 import concourse.mybir as mybir
+from concourse.masks import make_identity
 
 F32 = mybir.dt.float32
 BF16 = mybir.dt.bfloat16
@@ -23,6 +24,7 @@ SEAM = 2
 SCALAR_GROUPS = 30
 SCALAR_SCALINGS = 2
 ROOTS = 8192
+RAW = 16384
 SIGN_BIT = -(2**31)
 
 FLOPS = 2 * K * H * S + 2 * H * S * V
@@ -50,16 +52,24 @@ def tile_picked_ydec_as_p_kernel(
         e_tab = reuse.tile([P, W], I32, name="e_tab", align_bytes=64, offset=0)
         qn_tab = keep.tile([P, W], F32, name="qn_tab", align_bytes=64)
         mass_t = keep.tile([P, V], F32, name="mass_t")
-        own_t = reuse.tile([P, 64], F32, name="own_t", align_bytes=64, offset=4096)
-        five = keep.tile([P, P], F32, name="five")
-        w_raw = keep.tile([P, PACK, H], F32, name="w_raw")
+        own_rows = keep.tile([P, P], F32, name="own_rows")
+        ident = keep.tile([P, P], F32, name="ident")
+        five = [
+            reuse.tile([P, P], F32, name="five0", align_bytes=64, offset=4096),
+            keep.tile([P, P], F32, name="five1"),
+        ]
+        w_raw = reuse.tile([P, PACK, H], F32, name="w_raw", align_bytes=64, offset=RAW)
 
         nc.vector.memset(x_plane[:].bitcast(I32), 0)
         warm_in = keep.tile([P, 1], F32, name="warm_in")
         warm_out = keep.tile([P, 1], F32, name="warm_out")
         nc.vector.memset(warm_in[:], 1.0)
         nc.vector.memset(e_plane[:].bitcast(I32), 0)
-        nc.vector.memset(five[:], 5.0)
+        make_identity(nc, ident[:])
+        nc.gpsimd.memset(own_rows[:], 0.0)
+        nc.gpsimd.dma_start(out=own_rows[0:TILES, :], in_=own.rearrange("(n p) o -> n (p o)", p=P))
+        nc.vector.memset(five[0][:], 5.0)
+        nc.vector.memset(five[1][:], 5.0)
         w_rows = w1.rearrange("(p j) c -> p j c", j=PACK)
         nc.scalar.activation(out=warm_out[:], in_=warm_in[:], func=ACT.Abs_reciprocal_sqrt)
         nc.sync.dma_start(out=w_raw[:, :, 0:HALF], in_=w_rows[:, :, 0:HALF])
@@ -71,8 +81,6 @@ def tile_picked_ydec_as_p_kernel(
         load_scales(nc.sync, e_plane, e_scales)
         nc.sync.dma_start(cen_t[:], cen)
         nc.sync.dma_start(out=qn_tab[:], in_=qn)
-        with nc.allow_non_contiguous_dma(reason="one value a partition for each tile of samples"):
-            nc.sync.dma_start(out=own_t[:, 0:TILES], in_=own.rearrange("(n p) o -> p (n o)", p=P))
         nc.sync.dma_start(out=mass_t[:], in_=mass)
 
         x_sc = keep.tile([P, S], U8, name="x_sc", align_bytes=64)
@@ -159,7 +167,7 @@ def tile_picked_ydec_as_p_kernel(
                 stop=True,
             )
 
-        own5 = keep.tile([P, TILES], F32, name="own5")
+        own5 = reuse.tile([P, TILES], F32, name="own5", align_bytes=64, offset=RAW)
         q5 = keep.tile([P, V], F32, name="q5", align_bytes=64)
         den, root, inv, smass, gg = {}, {}, {}, {}, {}
         total = keep.tile([P, TILES], F32, name="total")
@@ -174,7 +182,7 @@ def tile_picked_ydec_as_p_kernel(
 
         def pick_norms(i):
             picked = qn_tab[:].indirect(cen_t[:, 8 * i : 8 * (i + 1)])
-            nc.vector.tensor_tensor(q5[:, i * P : (i + 1) * P], picked, five[:], ALU.mult)
+            nc.vector.tensor_tensor(q5[:, i * P : (i + 1) * P], picked, five[i][:], ALU.mult)
 
         def inverse_root(n):
             root[n] = reuse.tile([P, V], F32, name="root%d" % n, align_bytes=64, offset=ROOTS + 1024 * n)
@@ -222,9 +230,11 @@ def tile_picked_ydec_as_p_kernel(
                 nc.vector.tensor_scalar(res[:], gg[n][:], rtotal[n][:], None, ALU.mult)
             nc.sync.dma_start(out=out[n * P : (n + 1) * P, :], in_=res[:])
 
+        own_ps = psum.tile([P, P], F32, name="own_ps", offset=(2 * TILES - 1) * BANK)
+        nc.tensor.transpose(own_ps[:], own_rows[:], ident[:])
+        nc.scalar.activation(out=own5[:], in_=own_ps[:, 0:TILES], func=ACT.Copy, scale=5.0, bias=5.0)
         for n in range(TILES):
             first_product(n)
-        nc.gpsimd.tensor_scalar(own5[:], own_t[:, 0:TILES], 5.0, 5.0, ALU.mult, ALU.add)
         round_h(0)
         round_h(1)
         round_h(2)

@@ -24,15 +24,17 @@ SEAM = 2
 SCALAR_GROUPS = 30
 SCALAR_SCALINGS = 2
 ROOTS = 8192
+LATE = 13312
 RAW = 16384
+X_ROWS = 96
 SIGN_BIT = -(2**31)
 
 FLOPS = 2 * K * H * S + 2 * H * S * V
 
 
-def load_scales(queue, plane, scales):
+def place_scales(queue, plane, rows):
     for q in range(4):
-        queue.dma_start(out=plane[32 * q : 32 * q + 4, :].bitcast(I32), in_=scales[0, 4 * q : 4 * q + 4, :].bitcast(I32))
+        queue.dma_start(out=plane[32 * q : 32 * q + 4, :].bitcast(I32), in_=rows(q).bitcast(I32))
 
 
 def tile_picked_ydec_as_p_kernel(
@@ -47,44 +49,55 @@ def tile_picked_ydec_as_p_kernel(
         offs_t = keep.tile([P, S // 16], U16, name="offs_t")
         cen_t = keep.tile([P, V // 16], U16, name="cen_t")
         x_tab = keep.tile([P, T], I32, name="x_tab")
-        x_plane = keep.tile([P, T], U8, name="x_plane")
-        e_plane = keep.tile([P, W], U8, name="e_plane")
+        x_rows = keep.tile([P, T], U8, name="x_rows")
+        e_rows = keep.tile([P, W], U8, name="e_rows")
         e_tab = reuse.tile([P, W], I32, name="e_tab", align_bytes=64, offset=0)
         qn_tab = keep.tile([P, W], F32, name="qn_tab", align_bytes=64)
         mass_t = keep.tile([P, V], F32, name="mass_t")
         own_rows = keep.tile([P, P], F32, name="own_rows")
         ident = keep.tile([P, P], F32, name="ident")
         five = [
-            reuse.tile([P, P], F32, name="five0", align_bytes=64, offset=4096),
-            keep.tile([P, P], F32, name="five1"),
+            reuse.tile([P, P], F32, name="five0", align_bytes=64, offset=6144),
+            reuse.tile([P, P], F32, name="five1", align_bytes=64, offset=4096),
         ]
         w_raw = reuse.tile([P, PACK, H], F32, name="w_raw", align_bytes=64, offset=RAW)
+        x_pick = keep.tile([P, S], U8, name="x_pick")
+        e_pick = reuse.tile([P, V], U8, name="e_pick", align_bytes=64, offset=LATE)
+        x_sc = keep.tile([P, S], U8, name="x_sc", align_bytes=64)
+        e_sc = keep.tile([P, V], U8, name="e_sc", align_bytes=64)
 
-        nc.vector.memset(x_plane[:].bitcast(I32), 0)
         warm_in = keep.tile([P, 1], F32, name="warm_in")
         warm_out = keep.tile([P, 1], F32, name="warm_out")
         nc.vector.memset(warm_in[:], 1.0)
-        nc.vector.memset(e_plane[:].bitcast(I32), 0)
-        make_identity(nc, ident[:])
-        nc.gpsimd.memset(own_rows[:], 0.0)
-        nc.gpsimd.dma_start(out=own_rows[0:TILES, :], in_=own.rearrange("(n p) o -> n (p o)", p=P))
+        nc.vector.memset(e_rows[:].bitcast(I32), 0)
+        nc.vector.memset(own_rows[:], 0.0)
+        nc.vector.memset(x_rows[0:X_ROWS, :].bitcast(I32), 0)
+        nc.vector.memset(x_sc[:].bitcast(I32), 0)
+        nc.vector.memset(e_sc[:].bitcast(I32), 0)
         nc.vector.memset(five[0][:], 5.0)
         nc.vector.memset(five[1][:], 5.0)
+        make_identity(nc, ident[:])
         w_rows = w1.rearrange("(p j) c -> p j c", j=PACK)
         nc.scalar.activation(out=warm_out[:], in_=warm_in[:], func=ACT.Abs_reciprocal_sqrt)
-        nc.sync.dma_start(out=w_raw[:, :, 0:HALF], in_=w_rows[:, :, 0:HALF])
         nc.sync.dma_start(offs_t[:], offs)
-        load_scales(nc.sync, x_plane, x_scales)
+        nc.sync.dma_start(
+            out=x_rows[X_ROWS:P, :].bitcast(I32),
+            in_=x_scales[0].bitcast(I32).unsqueeze(1).broadcast_to([16, 2, T // 4]),
+        )
+        nc.sync.dma_start(out=w_raw[:, :, 0:HALF], in_=w_rows[:, :, 0:HALF])
+        nc.sync.dma_start(cen_t[:], cen)
+        nc.sync.dma_start(out=e_rows[0:16, :].bitcast(I32), in_=e_scales[0].bitcast(I32))
+        nc.sync.dma_start(out=own_rows[0:TILES, :], in_=own.rearrange("(n p) o -> n (p o)", p=P))
         nc.sync.dma_start(out=w_raw[:, :, HALF:H], in_=w_rows[:, :, HALF:H])
         nc.sync.dma_start(out=x_tab[:], in_=x_words[0].rearrange("p n t -> p (n t)").bitcast(I32))
-        nc.sync.dma_start(out=e_tab[:], in_=e_words[0].rearrange("p n t -> p (n t)").bitcast(I32))
-        load_scales(nc.sync, e_plane, e_scales)
-        nc.sync.dma_start(cen_t[:], cen)
-        nc.sync.dma_start(out=qn_tab[:], in_=qn)
-        nc.sync.dma_start(out=mass_t[:], in_=mass)
 
-        x_sc = keep.tile([P, S], U8, name="x_sc", align_bytes=64)
-        nc.vector.tensor_copy(x_sc[:], x_plane[:].indirect(offs_t[:]))
+        nc.vector.tensor_copy(x_pick[:], x_rows[:].indirect(offs_t[:]))
+        nc.vector.tensor_copy(e_pick[:], e_rows[:].indirect(cen_t[:]))
+        place_scales(nc.sync, x_sc, lambda q: x_pick[X_ROWS + 8 * q : X_ROWS + 8 * q + 8 : 2, :])
+        nc.sync.dma_start(out=e_tab[:], in_=e_words[0].rearrange("p n t -> p (n t)").bitcast(I32))
+        nc.sync.dma_start(out=qn_tab[:], in_=qn)
+        place_scales(nc.sync, e_sc, lambda q: e_pick[4 * q : 4 * q + 4, :])
+        nc.sync.dma_start(out=mass_t[:], in_=mass)
 
         w_codes = [keep.tile([P, P], U32, name="w_codes%d" % t, align_bytes=64) for t in range(PACK)]
         w_sc = [keep.tile([P, P], U8, name="w_sc%d" % t, align_bytes=64) for t in range(PACK)]
@@ -119,9 +132,7 @@ def tile_picked_ydec_as_p_kernel(
         pick_words(2, 2)
 
         e_codes = keep.tile([P, V], U32, name="e_codes", align_bytes=64)
-        e_sc = keep.tile([P, V], U8, name="e_sc", align_bytes=64)
         nc.vector.tensor_copy(e_codes[:], e_tab[:].bitcast(U32).indirect(cen_t[:]))
-        nc.vector.tensor_copy(e_sc[:], e_plane[:].indirect(cen_t[:]))
 
         h_ps, h_bf = {}, {}
 
@@ -139,10 +150,7 @@ def tile_picked_ydec_as_p_kernel(
                 )
 
         def round_h(n):
-            if n == 1:
-                h_bf[n] = reuse.tile([P, P, PACK], BF16, name="h_bf%d" % n, align_bytes=64, offset=6144)
-            else:
-                h_bf[n] = keep.tile([P, P, PACK], BF16, name="h_bf%d" % n, align_bytes=64)
+            h_bf[n] = keep.tile([P, P, PACK], BF16, name="h_bf%d" % n, align_bytes=64)
             nc.scalar.copy(
                 out=h_bf[n][:].rearrange("p (c i) t -> p c t i", i=2),
                 in_=h_ps[n][:].rearrange("p t (c i) -> p c t i", i=2),
@@ -152,7 +160,7 @@ def tile_picked_ydec_as_p_kernel(
 
         def second_product(n):
             h_codes = keep.tile([P, P], U32, name="h_codes%d" % n, align_bytes=64)
-            h_sc = reuse.tile([P, P], U8, name="h_sc%d" % n, align_bytes=64, offset=(0, 4096, 6144, 6144 + 128)[n])
+            h_sc = reuse.tile([P, P], U8, name="h_sc%d" % n, align_bytes=64, offset=(0, 6144, 4096, 4096 + 128)[n])
             nc.vector.quantize_mx(
                 out=h_codes[:].bitcast(FP8X4), scales=h_sc[:], in_=h_bf[n][:].rearrange("p n t -> p (n t)")
             )
@@ -168,7 +176,7 @@ def tile_picked_ydec_as_p_kernel(
             )
 
         own5 = reuse.tile([P, TILES], F32, name="own5", align_bytes=64, offset=RAW)
-        q5 = keep.tile([P, V], F32, name="q5", align_bytes=64)
+        q5 = reuse.tile([P, V], F32, name="q5", align_bytes=64, offset=LATE)
         den, root, inv, smass, gg = {}, {}, {}, {}, {}
         total = keep.tile([P, TILES], F32, name="total")
         rtotal = {}

@@ -51,7 +51,7 @@ def tile_picked_ydec_as_p_kernel(
         x_tab = keep.tile([P, T], I32, name="x_tab")
         x_rows = keep.tile([P, T], U8, name="x_rows")
         e_rows = keep.tile([P, W], U8, name="e_rows")
-        e_tab = reuse.tile([P, W], I32, name="e_tab", align_bytes=64, offset=0)
+        e_tab = keep.tile([P, W], I32, name="e_tab", align_bytes=64)
         qn_tab = keep.tile([P, W], F32, name="qn_tab", align_bytes=64)
         mass_t = keep.tile([P, V], F32, name="mass_t")
         own_rows = keep.tile([P, P], F32, name="own_rows")
@@ -93,8 +93,10 @@ def tile_picked_ydec_as_p_kernel(
 
         nc.vector.tensor_copy(x_pick[:], x_rows[:].indirect(offs_t[:]))
         nc.vector.tensor_copy(e_pick[:], e_rows[:].indirect(cen_t[:]))
+        e_src = e_words[0].rearrange("p n t -> p (n t)").bitcast(I32)
+        nc.sync.dma_start(out=e_tab[:, 0 : W // 2], in_=e_src[:, 0 : W // 2])
         place_scales(nc.sync, x_sc, lambda q: x_pick[X_ROWS + 8 * q : X_ROWS + 8 * q + 8 : 2, :])
-        nc.sync.dma_start(out=e_tab[:], in_=e_words[0].rearrange("p n t -> p (n t)").bitcast(I32))
+        nc.sync.dma_start(out=e_tab[:, W // 2 : W], in_=e_src[:, W // 2 : W])
         nc.sync.dma_start(out=qn_tab[:], in_=qn)
         place_scales(nc.sync, e_sc, lambda q: e_pick[4 * q : 4 * q + 4, :])
         nc.sync.dma_start(out=mass_t[:], in_=mass)
@@ -137,10 +139,15 @@ def tile_picked_ydec_as_p_kernel(
         h_ps, h_bf = {}, {}
 
         def first_product(n):
-            h_ps[n] = psum.tile([P, PACK, P], F32, name="h_ps%d" % n, offset=n * BANK)
+            if n == 0:
+                h_ps[n] = [psum.tile([P, 2, P], F32, name="h_ps0_%d" % u, offset=(0, 7 * BANK)[u]) for u in range(2)]
+                parts = [h_ps[n][t // 2][:, t % 2, :] for t in range(PACK)]
+            else:
+                h_ps[n] = psum.tile([P, PACK, P], F32, name="h_ps%d" % n, offset=n * BANK)
+                parts = [h_ps[n][:, t, :] for t in range(PACK)]
             for t in range(PACK):
                 nc.tensor.matmul_mx(
-                    out=h_ps[n][:, t, :],
+                    out=parts[t],
                     lhsT=w_codes[t][:].bitcast(FP8X4),
                     lhsT_scale=w_sc[t][:],
                     rhs=x_codes[n].bitcast(FP8X4),
@@ -151,10 +158,13 @@ def tile_picked_ydec_as_p_kernel(
 
         def round_h(n):
             h_bf[n] = keep.tile([P, P, PACK], BF16, name="h_bf%d" % n, align_bytes=64)
-            nc.scalar.copy(
-                out=h_bf[n][:].rearrange("p (c i) t -> p c t i", i=2),
-                in_=h_ps[n][:].rearrange("p t (c i) -> p c t i", i=2),
-            )
+            dst = h_bf[n][:].rearrange("p (c i) t -> p c t i", i=2)
+            if n == 0:
+                src = [part[:].rearrange("p t (c i) -> p c t i", i=2) for part in h_ps[n]]
+                nc.vector.tensor_copy(out=dst[:, :, 0:2], in_=src[0])
+                nc.scalar.copy(out=dst[:, :, 2:4], in_=src[1])
+            else:
+                nc.scalar.copy(out=dst, in_=h_ps[n][:].rearrange("p t (c i) -> p c t i", i=2))
 
         y_ps = {}
 

@@ -48,23 +48,23 @@ def tile_picked_ydec_as_p_kernel(
 
         offs_t = keep.tile([P, S // 16], U16, name="offs_t")
         cen_t = keep.tile([P, V // 16], U16, name="cen_t")
-        x_tab = keep.tile([P, T], I32, name="x_tab")
-        x_rows = keep.tile([P, T], U8, name="x_rows")
-        e_rows = keep.tile([P, W], U8, name="e_rows")
-        e_tab = keep.tile([P, W], I32, name="e_tab", align_bytes=64)
-        qn_tab = keep.tile([P, W], F32, name="qn_tab", align_bytes=64)
-        mass_t = keep.tile([P, V], F32, name="mass_t")
-        own_rows = keep.tile([P, P], F32, name="own_rows")
+        x_tab = keep.tile([P, T], I32, name="x_tab", align_bytes=256)
+        x_rows = keep.tile([P, T], U8, name="x_rows", align_bytes=256)
+        e_rows = keep.tile([P, W], U8, name="e_rows", align_bytes=256)
+        e_tab = keep.tile([P, W], I32, name="e_tab", align_bytes=256)
+        qn_tab = keep.tile([P, W], F32, name="qn_tab", align_bytes=256)
+        mass_t = keep.tile([P, V], F32, name="mass_t", align_bytes=256)
+        own_rows = keep.tile([P, P], F32, name="own_rows", align_bytes=256)
         ident = keep.tile([P, P], F32, name="ident")
         five = [
             reuse.tile([P, P], F32, name="five0", align_bytes=64, offset=6144),
             reuse.tile([P, P], F32, name="five1", align_bytes=64, offset=4096),
         ]
-        w_raw = reuse.tile([P, PACK, H], F32, name="w_raw", align_bytes=64, offset=RAW)
-        x_pick = keep.tile([P, S], U8, name="x_pick")
+        w_raw = reuse.tile([P, PACK, H], F32, name="w_raw", align_bytes=256, offset=RAW)
+        x_pick = keep.tile([P, S], U8, name="x_pick", align_bytes=256)
         e_pick = reuse.tile([P, V], U8, name="e_pick", align_bytes=64, offset=LATE)
-        x_sc = keep.tile([P, S], U8, name="x_sc", align_bytes=64)
-        e_sc = keep.tile([P, V], U8, name="e_sc", align_bytes=64)
+        x_sc = keep.tile([P, S], U8, name="x_sc", align_bytes=256)
+        e_sc = keep.tile([P, V], U8, name="e_sc", align_bytes=256)
 
         warm_in = keep.tile([P, 1], F32, name="warm_in")
         warm_out = keep.tile([P, 1], F32, name="warm_out")
@@ -239,9 +239,9 @@ def tile_picked_ydec_as_p_kernel(
 
         def normalise(n):
             if n == 0:
-                res = reuse.tile([P, V], F32, name="res%d" % n, align_bytes=64, offset=ROOTS + 3072 + 64)
+                res = reuse.tile([P, V], F32, name="res%d" % n, align_bytes=256, offset=ROOTS + 3072 + 256)
             else:
-                res = keep.tile([P, V], F32, name="res%d" % n)
+                res = keep.tile([P, V], F32, name="res%d" % n, align_bytes=256)
             if n < SCALAR_SCALINGS:
                 nc.scalar.activation(out=res[:], in_=gg[n][:], func=ACT.Copy, scale=rtotal[n][:])
             else:

from contextlib import ExitStack

import concourse.mybir as mybir
from concourse.masks import make_identity

F32 = mybir.dt.float32
BF16 = mybir.dt.bfloat16
I32 = mybir.dt.int32
U32 = mybir.dt.uint32
U16 = mybir.dt.uint16
U8 = mybir.dt.uint8
FP8X4 = mybir.dt.float8_e4m3fn_x4
ALU = mybir.AluOpType
ACT = mybir.ActivationFunctionType

P = 128
PACK = 4
K, T, S, H, V, W = 512, 1024, 512, 512, 256, 1024
TILES = S // P
HALF = H // 2
GROUPS = HALF // PACK
BANK = 2048
SEAM = 2
SCALAR_GROUPS = 30
SCALAR_SCALINGS = 2
ROOTS = 8192
LATE = 13312
RAW = 16384
X_ROWS = 96
SIGN_BIT = -(2**31)

FLOPS = 2 * K * H * S + 2 * H * S * V


def place_scales(queue, plane, rows):
    for q in range(4):
        queue.dma_start(out=plane[32 * q : 32 * q + 4, :].bitcast(I32), in_=rows(q).bitcast(I32))


def tile_picked_ydec_as_p_kernel(
    tc, x_words, x_scales, w1, e_words, e_scales, qn, own, mass, offs, cen, out
):
    nc = tc.nc
    with ExitStack() as ctx:
        keep = ctx.enter_context(tc.tile_pool(name="keep", bufs=1))
        reuse = ctx.enter_context(tc.tile_pool(name="reuse", bufs=1))
        psum = ctx.enter_context(tc.psum_pool(name="psum", bufs=1))

        offs_t = keep.tile([P, S // 16], U16, name="offs_t")
        cen_t = keep.tile([P, V // 16], U16, name="cen_t")
        x_tab = keep.tile([P, T], I32, name="x_tab", align_bytes=256)
        x_rows = keep.tile([P, T], U8, name="x_rows", align_bytes=256)
        e_rows = keep.tile([P, W], U8, name="e_rows", align_bytes=256)
        e_tab = keep.tile([P, W], I32, name="e_tab", align_bytes=256)
        qn_tab = keep.tile([P, W], F32, name="qn_tab", align_bytes=256)
        mass_t = keep.tile([P, V], F32, name="mass_t", align_bytes=256)
        own_rows = keep.tile([P, P], F32, name="own_rows", align_bytes=256)
        ident = keep.tile([P, P], F32, name="ident")
        five = [
            reuse.tile([P, P], F32, name="five0", align_bytes=64, offset=6144),
            reuse.tile([P, P], F32, name="five1", align_bytes=64, offset=4096),
        ]
        w_raw = reuse.tile([P, PACK, H], F32, name="w_raw", align_bytes=256, offset=RAW)
        x_pick = keep.tile([P, S], U8, name="x_pick", align_bytes=256)
        e_pick = reuse.tile([P, V], U8, name="e_pick", align_bytes=64, offset=LATE)
        x_sc = keep.tile([P, S], U8, name="x_sc", align_bytes=256)
        e_sc = keep.tile([P, V], U8, name="e_sc", align_bytes=256)

        warm_in = keep.tile([P, 1], F32, name="warm_in")
        warm_out = keep.tile([P, 1], F32, name="warm_out")
        nc.vector.memset(warm_in[:], 1.0)
        nc.vector.memset(e_rows[:].bitcast(I32), 0)
        nc.vector.memset(own_rows[:], 0.0)
        nc.vector.memset(x_rows[0:X_ROWS, :].bitcast(I32), 0)
        nc.vector.memset(x_sc[:].bitcast(I32), 0)
        nc.vector.memset(e_sc[:].bitcast(I32), 0)
        nc.vector.memset(five[0][:], 5.0)
        nc.vector.memset(five[1][:], 5.0)
        make_identity(nc, ident[:])
        w_rows = w1.rearrange("(p j) c -> p j c", j=PACK)
        nc.scalar.activation(out=warm_out[:], in_=warm_in[:], func=ACT.Abs_reciprocal_sqrt)
        nc.sync.dma_start(offs_t[:], offs)
        nc.sync.dma_start(
            out=x_rows[X_ROWS:P, :].bitcast(I32),
            in_=x_scales[0].bitcast(I32).unsqueeze(1).broadcast_to([16, 2, T // 4]),
        )
        nc.sync.dma_start(out=w_raw[:, :, 0:HALF], in_=w_rows[:, :, 0:HALF])
        nc.sync.dma_start(cen_t[:], cen)
        nc.sync.dma_start(out=e_rows[0:16, :].bitcast(I32), in_=e_scales[0].bitcast(I32))
        nc.sync.dma_start(out=own_rows[0:TILES, :], in_=own.rearrange("(n p) o -> n (p o)", p=P))
        nc.sync.dma_start(out=w_raw[:, :, HALF:H], in_=w_rows[:, :, HALF:H])
        nc.sync.dma_start(out=x_tab[:], in_=x_words[0].rearrange("p n t -> p (n t)").bitcast(I32))

        nc.vector.tensor_copy(x_pick[:], x_rows[:].indirect(offs_t[:]))
        nc.vector.tensor_copy(e_pick[:], e_rows[:].indirect(cen_t[:]))
        e_src = e_words[0].rearrange("p n t -> p (n t)").bitcast(I32)
        nc.sync.dma_start(out=e_tab[:, 0 : W // 2], in_=e_src[:, 0 : W // 2])
        place_scales(nc.sync, x_sc, lambda q: x_pick[X_ROWS + 8 * q : X_ROWS + 8 * q + 8 : 2, :])
        nc.sync.dma_start(out=e_tab[:, W // 2 : W], in_=e_src[:, W // 2 : W])
        nc.sync.dma_start(out=qn_tab[:], in_=qn)
        place_scales(nc.sync, e_sc, lambda q: e_pick[4 * q : 4 * q + 4, :])
        nc.sync.dma_start(out=mass_t[:], in_=mass)

        w_codes = [keep.tile([P, P], U32, name="w_codes%d" % t, align_bytes=64) for t in range(PACK)]
        w_sc = [keep.tile([P, P], U8, name="w_sc%d" % t, align_bytes=64) for t in range(PACK)]
        w_bf = keep.tile([P, PACK, P, PACK], BF16, name="w_bf", align_bytes=64)
        w_dst = w_bf[:].rearrange("p t m j -> p m j t")
        w_src = w_raw[:].rearrange("p j (m t) -> p m j t", t=PACK)
        cuts = (0, GROUPS - SEAM, GROUPS + SEAM, GROUPS + SCALAR_GROUPS)
        for lo, hi in zip(cuts, cuts[1:]):
            nc.scalar.copy(out=w_dst[:, lo:hi], in_=w_src[:, lo:hi])
        nc.vector.tensor_copy(out=w_dst[:, cuts[-1] : P], in_=w_src[:, cuts[-1] : P])

        def quantise_half(i):
            cols = slice(i * GROUPS, (i + 1) * GROUPS)
            for t in range(PACK):
                nc.vector.quantize_mx(
                    out=w_codes[t][:, cols].bitcast(FP8X4),
                    scales=w_sc[t][:, cols],
                    in_=w_bf[:, t, cols].rearrange("p m j -> p (m j)"),
                )

        x_codes = []

        def pick_words(first, count):
            picked = keep.tile([P, count * P], U32, name="x_codes%d" % first, align_bytes=64)
            nc.vector.tensor_copy(picked[:], x_tab[:].bitcast(U32).indirect(offs_t[:, 8 * first : 8 * (first + count)]))
            x_codes.extend(picked[:, i * P : (i + 1) * P] for i in range(count))

        quantise_half(0)
        quantise_half(1)
        pick_words(0, 1)
        pick_words(1, 1)
        pick_words(2, 2)

        e_codes = keep.tile([P, V], U32, name="e_codes", align_bytes=64)
        nc.vector.tensor_copy(e_codes[:], e_tab[:].bitcast(U32).indirect(cen_t[:]))

        h_ps, h_bf = {}, {}

        def first_product(n):
            if n == 0:
                h_ps[n] = [psum.tile([P, 2, P], F32, name="h_ps0_%d" % u, offset=(0, 7 * BANK)[u]) for u in range(2)]
                parts = [h_ps[n][t // 2][:, t % 2, :] for t in range(PACK)]
            else:
                h_ps[n] = psum.tile([P, PACK, P], F32, name="h_ps%d" % n, offset=n * BANK)
                parts = [h_ps[n][:, t, :] for t in range(PACK)]
            for t in range(PACK):
                nc.tensor.matmul_mx(
                    out=parts[t],
                    lhsT=w_codes[t][:].bitcast(FP8X4),
                    lhsT_scale=w_sc[t][:],
                    rhs=x_codes[n].bitcast(FP8X4),
                    rhs_scale=x_sc[:, n * P : (n + 1) * P],
                    start=True,
                    stop=True,
                )

        def round_h(n):
            h_bf[n] = keep.tile([P, P, PACK], BF16, name="h_bf%d" % n, align_bytes=64)
            dst = h_bf[n][:].rearrange("p (c i) t -> p c t i", i=2)
            if n == 0:
                src = [part[:].rearrange("p t (c i) -> p c t i", i=2) for part in h_ps[n]]
                nc.vector.tensor_copy(out=dst[:, :, 0:2], in_=src[0])
                nc.scalar.copy(out=dst[:, :, 2:4], in_=src[1])
            else:
                nc.scalar.copy(out=dst, in_=h_ps[n][:].rearrange("p t (c i) -> p c t i", i=2))

        y_ps = {}

        def second_product(n):
            h_codes = keep.tile([P, P], U32, name="h_codes%d" % n, align_bytes=64)
            h_sc = reuse.tile([P, P], U8, name="h_sc%d" % n, align_bytes=64, offset=(0, 6144, 4096, 4096 + 128)[n])
            nc.vector.quantize_mx(
                out=h_codes[:].bitcast(FP8X4), scales=h_sc[:], in_=h_bf[n][:].rearrange("p n t -> p (n t)")
            )
            y_ps[n] = psum.tile([P, V], F32, name="y_ps%d" % n, offset=(TILES + n) * BANK)
            nc.tensor.matmul_mx(
                out=y_ps[n][:],
                lhsT=h_codes[:].bitcast(FP8X4),
                lhsT_scale=h_sc[:],
                rhs=e_codes[:].bitcast(FP8X4),
                rhs_scale=e_sc[:],
                start=True,
                stop=True,
            )

        own5 = reuse.tile([P, TILES], F32, name="own5", align_bytes=64, offset=RAW)
        q5 = reuse.tile([P, V], F32, name="q5", align_bytes=64, offset=LATE)
        den, root, inv, smass, gg = {}, {}, {}, {}, {}
        total = keep.tile([P, TILES], F32, name="total")
        rtotal = {}

        def denominator(n, cols=slice(0, V)):
            if n not in den:
                den[n] = keep.tile([P, V], F32, name="den%d" % n)
            nc.vector.scalar_tensor_tensor(
                den[n][:, cols], y_ps[n][:, cols], own5[:, n : n + 1], q5[:, cols], ALU.subtract, ALU.subtract
            )

        def pick_norms(i):
            picked = qn_tab[:].indirect(cen_t[:, 8 * i : 8 * (i + 1)])
            nc.vector.tensor_tensor(q5[:, i * P : (i + 1) * P], picked, five[i][:], ALU.mult)

        def inverse_root(n):
            root[n] = reuse.tile([P, V], F32, name="root%d" % n, align_bytes=64, offset=ROOTS + 1024 * n)
            nc.scalar.activation(out=root[n][:], in_=den[n][:], func=ACT.Abs_reciprocal_sqrt)

        def square(n):
            inv[n] = keep.tile([P, V], F32, name="inv%d" % n)
            nc.scalar.activation(out=inv[n][:], in_=root[n][:], func=ACT.Square)

        def signed_mass(n):
            if n >= 2:
                smass[n] = reuse.tile([P, V], F32, name="smass%d" % n, align_bytes=64, offset=ROOTS + 1024 * (n - 2))
            else:
                smass[n] = keep.tile([P, V], F32, name="smass%d" % n)
            nc.vector.scalar_tensor_tensor(
                smass[n][:].bitcast(I32),
                den[n][:].bitcast(I32),
                SIGN_BIT,
                mass_t[:].bitcast(I32),
                ALU.bitwise_and,
                ALU.bitwise_xor,
            )

        def weight(n):
            gg[n] = keep.tile([P, V], F32, name="gg%d" % n)
            nc.vector.scalar_tensor_tensor(
                gg[n][:], inv[n][:], 1.0, smass[n][:], ALU.mult, ALU.mult, accum_out=total[:, n : n + 1]
            )

        def invert_total(n):
            if n == 2:
                rtotal[n] = reuse.tile([P, 1], F32, name="rtotal%d" % n, align_bytes=64, offset=ROOTS + 3072)
            else:
                rtotal[n] = keep.tile([P, 1], F32, name="rtotal%d" % n)
            nc.vector.reciprocal(rtotal[n][:], total[:, n : n + 1])

        def normalise(n):
            if n == 0:
                res = reuse.tile([P, V], F32, name="res%d" % n, align_bytes=256, offset=ROOTS + 3072 + 256)
            else:
                res = keep.tile([P, V], F32, name="res%d" % n, align_bytes=256)
            if n < SCALAR_SCALINGS:
                nc.scalar.activation(out=res[:], in_=gg[n][:], func=ACT.Copy, scale=rtotal[n][:])
            else:
                nc.vector.tensor_scalar(res[:], gg[n][:], rtotal[n][:], None, ALU.mult)
            nc.sync.dma_start(out=out[n * P : (n + 1) * P, :], in_=res[:])

        own_ps = psum.tile([P, P], F32, name="own_ps", offset=(2 * TILES - 1) * BANK)
        nc.tensor.transpose(own_ps[:], own_rows[:], ident[:])
        nc.scalar.activation(out=own5[:], in_=own_ps[:, 0:TILES], func=ACT.Copy, scale=5.0, bias=5.0)
        for n in range(TILES):
            first_product(n)
        round_h(0)
        round_h(1)
        round_h(2)
        round_h(3)
        second_product(0)
        pick_norms(0)
        pick_norms(1)
        second_product(1)
        denominator(0, slice(0, P))
        denominator(0, slice(P, V))
        second_product(2)
        second_product(3)
        denominator(1)
        signed_mass(0)
        denominator(2)
        denominator(3)
        signed_mass(1)
        inverse_root(0)
        inverse_root(1)
        square(0)
        inverse_root(2)
        square(1)
        inverse_root(3)
        square(2)
        square(3)
        weight(0)
        signed_mass(2)
        invert_total(0)
        weight(1)
        signed_mass(3)
        invert_total(1)
        weight(2)
        weight(3)
        invert_total(2)
        normalise(0)
        normalise(1)
        invert_total(3)
        normalise(2)
        normalise(3)
